import numpy as np, ml_dtypes
CORES = [48,51,52,55]
N = 4
BF = ml_dtypes.bfloat16
M, Q, CAP, V = 4096, 384, 160, 16
R = 2 ** 20; H = R - 2 ** 13
def shave(lo, hi, u, k):
    return [lo[i] + int((hi[i] - lo[i]) * k * u[3 + i]) for i in range(3)] + [hi[i] - int((hi[i] - lo[i]) * k * u[6 + i]) for i in range(3)]
def scene(rng, h, deep, uneven):
    U = rng.random((M, 12)).tolist(); u = U[0]; side = [int(h * (1 + 0.5 * u[i])) for i in range(3)]
    lo = [int(u[3 + i] * (2 * h - side[i])) - h for i in range(3)]; hi = [lo[i] + side[i] for i in range(3)]
    box = [lo + hi] * M; skip = [M] * M; todo = [(1, M, lo, hi, M, V - 1)]
    while todo:
        a, b, lo, hi, out, v = todo.pop(); u = U[a]; s = b - a
        if s <= 4 or (s <= v and (deep or u[0] < 0.3)):
            for n in range(a, b):
                w = U[n]; box[n] = shave(lo, hi, w, 0.25)
                k = n + 1 if deep or w[2] < 0.5 else n + 1 + int(w[11] * (b - n)); skip[n] = k if k < b else out
            if out > b:
                i = int(u[1] * 3); box[b - 1][3 + i] = box[b - 1][i] - 1
            continue
        c = 5 * 2 ** (v - 5) - 1; x = max(2, s - 1 - c); z = min(s - 3, c)
        m = a + 1 + (V - 2 if deep and a == 1 else x + int(u[9] * (z - x + 1)))
        i = int(u[1] * 3); cut = lo[i] + int((hi[i] - lo[i]) * (0.25 + 0.5 * u[10]))
        l2 = lo[:]; l2[i] = min(cut + 1, hi[i]); h2 = hi[:]; h2[i] = cut
        yes, no = ((lo, h2), (l2, hi)) if u[2] < 0.5 else ((l2, hi), (lo, h2))
        box[a] = shave(yes[0], yes[1], u, 0.125); skip[a] = m
        todo += [(a + 1, m) + yes + (out, v - 1), (m, b) + no + (out, v - 1)]
    w = 2 ** rng.integers(0, 17, M) if uneven else rng.integers(1, 2 ** 16 + 1, M)
    return np.concatenate([np.array(box, np.int64).T, np.array([skip], np.int64), (w * (2 * rng.integers(0, 2, M) - 1))[None]])
def scenes(rng, h, deep=False, uneven=False):
    t = np.zeros((N, 8, 16, M), np.int64)
    for r in range(N):
        for g in range(8):
            t[r, g, :8] = scene(rng, int(h[g]), deep, uneven)
    return t
def points(rng, h):
    h = np.asarray(h, np.int64).reshape(1, 8, 1, 1); return rng.integers(-h, h + 1, (N, 8, 3, Q))
def inbox(t, p):
    return ((t[:, :3, :1] <= p) & (p <= t[:, 3:6, :1])).all(-2)
def far(rng, n):
    return rng.integers(R - 2 ** 12, R + 1, (3, n))
def made(rng, t, p, s=0):
    for r in range(N):
        for q in [(r + s + i) % N for i in range(N)]:
            if q == r: continue
            k = inbox(t[q], p[r])
            for g in range(8):
                i = rng.permutation(np.flatnonzero(k[g]))[CAP:]
                if len(i): p[r, g][:, i] = far(rng, len(i))
    return {"nodes": t.reshape(N, 128, M).astype(np.int32), "pts": p.reshape(N, 24, Q).astype(np.int32)}
def setup_inputs(rng):
    return made(rng, scenes(rng, [H] * 8), points(rng, [H] * 8))
def setup_inputs_faces(rng):
    t = scenes(rng, [H] * 8); p = np.zeros((N, 8, 3, Q), np.int64)
    for g in range(8):
        q = rng.integers(0, N, (N, 1, Q)); n = rng.integers(0, M, (N, 1, Q)) * (rng.random((N, 1, Q)) > 0.25)
        p[:, g] = t[q, g, np.arange(3)[:, None] + 3 * rng.integers(0, 2, (N, 3, Q)), n] + rng.integers(-1, 2, (N, 3, Q))
    return made(rng, t, p)
def setup_inputs_full(rng):
    t = scenes(rng, [H] * 8); p = points(rng, [H] * 8); s = int(rng.integers(1, N))
    for r in range(N):
        b = t[(r + s) % N, :, :6, :1]; p[r] = b[:, :3] + np.floor(rng.random((8, 3, Q)) * (b[:, 3:] - b[:, :3] + 1)).astype(np.int64)
    return made(rng, t, p, s)
def setup_inputs_few(rng):
    t = scenes(rng, [H] * 8); p = points(rng, [H] * 8); o = rng.permutation(N); b, c = o[:2]; e = o[2:]; t[e, :, 3, 0] = t[e, :, 0, 0] - 1
    w = t[c, :, :6, :1]; p[c] = w[:, :3] + np.floor(rng.random((8, 3, Q)) * (w[:, 3:] - w[:, :3] + 1)).astype(np.int64)
    for g in range(8):
        p[b, g] = far(rng, Q); v = t[b, g, :3, 0] + np.floor(rng.random(3) * (t[b, g, 3:6, 0] - t[b, g, :3, 0] + 1)).astype(np.int64)
        p[b, g, :, :4] = v[:, None]; p[b, g, :, Q - 4:] = v[:, None]
    return made(rng, t, p)
def setup_inputs_deep(rng):
    return made(rng, scenes(rng, [H] * 8, deep=True), points(rng, [H] * 8))
def setup_inputs_spread(rng):
    h = 2 ** rng.integers(5, 20, 8); p = points(rng, h)
    return made(rng, scenes(rng, h, uneven=True), p >> (rng.integers(0, 6, (N, 8, 1, Q)) * (rng.random((N, 8, 1, Q)) < 0.25)))
def walk(t, p):
    nd = t.transpose(0, 2, 1); x = p.transpose(0, 1, 3, 2); c = np.zeros((N, 8, Q), np.int64); s = np.zeros_like(c); v = np.zeros_like(c)
    while (c < M).any():
        live = c < M; b = nd[np.arange(8)[:, None], np.minimum(c, M - 1)]
        hit = live & (b[..., :3] <= x).all(-1) & (x <= b[..., 3:6]).all(-1)
        s += hit * b[..., 7]; v += live; c = np.where(live, np.where(hit, c + 1, b[..., 6]), c)
    return s, v
def check_inputs(d):
    t = d["nodes"].astype(np.int64).reshape(N, 8, 16, M); p = d["pts"].astype(np.int64).reshape(N, 8, 3, Q); k = t[:, :, 6]; bad = []
    if (k <= np.arange(M)).any() or (k > M).any() or (k[:, :, 0] != M).any(): return ["skips"]
    if np.abs(t[:, :, :6]).max() > R or np.abs(p).max() > R: bad.append("coordinates")
    if np.abs(t[:, :, 7]).max() > 2 ** 16: bad.append("weights")
    if t[:, :, 8:].any(): bad.append("rows of zeros")
    n = np.stack([np.sum(inbox(t[q], p), axis=-1) for q in range(N)])
    n[np.arange(N), np.arange(N)] = 0
    if n.max() > CAP: bad.append("points in another rank's first box")
    if max(walk(t[q], p)[1].max() for q in range(N)) > V: bad.append("visits")
    return bad
def reference(nodes, pts):
    t = nodes.astype(np.int64).reshape(N, 8, 16, M); p = pts.astype(np.int64).reshape(N, 8, 3, Q); y = np.zeros((N, 8, Q), np.int64)
    for q in range(N):
        y += walk(t[q], p)[0]
    return {"y": y.astype(np.float32)}

@@ -1,0 +1,427 @@
+from concourse.bass import DstId, RemoteDMATransfer
+from concourse.mybir import dt, AluOpType, AxisListType, ActivationFunctionType
+
+OP = AluOpType
+FN = ActivationFunctionType
+NB = 3
+NL = 512
+STEPS = 15
+M = 4096
+WIN = 4104
+WIN2 = 4112
+WC = 4
+EPD = 4
+BIG = 262144.0
+TOP = 57344.0
+
+SCRATCH = {
+    "W": ("sbuf", [128, WIN], "int32"),
+    "W2": ("sbuf", [128, WIN2], "bfloat16"),
+    "Z": ("sbuf", [128, 512], "bfloat16"),
+    "X": ("dram", [128, 96], "int32"),
+    "N0": ("sbuf", [128, 2], "int32"),
+    "KV": ("sbuf", [128, 4], "bfloat16"),
+    "P": ("sbuf", [128, NB * NL], "int32"),
+    "CM": ("sbuf", [128, 128], "float32"),
+    "CQ": ("sbuf", [128, 128], "float32"),
+    "X2": ("sbuf", [128, 512], "int32"),
+    "HI": ("sbuf", [128, 512], "bfloat16"),
+    "LO": ("sbuf", [128, 512], "bfloat16"),
+    "NHB": ("sbuf", [128, 512], "bfloat16"),
+    "NLB": ("sbuf", [128, 512], "bfloat16"),
+    "PR": ("sbuf", [128, 4 * 384], "int32"),
+    "CI": ("sbuf", [128, 128], "int32"),
+    "CJ": ("sbuf", [128, 128], "int32"),
+    "CG": ("sbuf", [128, 32], "int32"),
+    "CH": ("sbuf", [128, 32], "int32"),
+    "KI": ("sbuf", [128, 16], "int32"),
+    "KB": ("sbuf", [128, 8], "float32"),
+    "KF": ("sbuf", [128, 64], "float32"),
+    "ID": ("sbuf", [128, 128], "bfloat16"),
+    "NID": ("sbuf", [128, 128], "bfloat16"),
+    "IDF": ("sbuf", [128, 128], "float32"),
+    "MASK": ("sbuf", [128, 128], "float32"),
+    "FIT": ("sbuf", [128, 256], "float32"),
+    "B32": ("sbuf", [128, 32], "float32"),
+    "B8": ("sbuf", [128, 32], "float32"),
+    "SEL": ("sbuf", [128, 32], "float16"),
+    "NSEL": ("sbuf", [128, 32], "float16"),
+    "RA": ("sbuf", [128, 96], "bfloat16"),
+    "RB": ("sbuf", [128, 64], "bfloat16"),
+    "R0": ("sbuf", [128, 128], "bfloat16"),
+    "R1": ("sbuf", [128, 96], "bfloat16"),
+    "OUT": ("sbuf", [128, 96], "float32"),
+    "TMP": ("sbuf", [128, 96], "float32"),
+    "SUM": ("sbuf", [128, 24], "float32"),
+    "YS": ("sbuf", [128, 128], "float32"),
+    "AC0": ("psum", [128, 512], "float32"),
+    "AC1": ("psum", [128, 512], "float32"),
+}
+for _b in range(NB):
+    SCRATCH["C%d" % _b] = ("sbuf", [128, NL], "bfloat16")
+    SCRATCH["G%d" % _b] = ("sbuf", [128, NL], "bfloat16")
+    SCRATCH["CU%d" % _b] = ("sbuf", [128, 32], "uint16")
+    SCRATCH["IN%d" % _b] = ("sbuf", [128, 256], "float16")
+    SCRATCH["HW%d" % _b] = ("sbuf", [128, 128], "bfloat16")
+    SCRATCH["HX%d" % _b] = ("sbuf", [128, 128], "bfloat16")
+    SCRATCH["BK%d" % _b] = ("psum", [128, 512], "float32")
+    SCRATCH["CP%d" % _b] = ("psum", [128, 512], "float32")
+for _r in range(4):
+    SCRATCH["D%d" % _r] = ("dram", [128, 96], "int32")
+    SCRATCH["L%d" % _r] = ("sbuf", [128, 24], "float32")
+
+SEMAPHORES = ["xld", "x2ld", "fill", "fz", "f2", "fp", "v", "iot", "w2ld", "own", "psent", "rsent",
+              "lo", "oa", "fin", "fq", "yd", "hl", "n0", "nb", "go", "kv", "rr", "rs"]
+SEMAPHORES += ["fw%d" % c for c in range(WC)] + ["wl%d" % c for c in range(WC)]
+for _b in range(NB):
+    SEMAPHORES += ["%s%d" % (n, _b) for n in ("cu", "cc", "gg", "mm", "mn", "ee", "hw", "ac")]
+for _r in range(4):
+    SEMAPHORES += ["pa%d" % _r, "pl%d" % _r, "ra%d" % _r]
+
+
+def rank_program(g, core, T, topo):
+    rank = T.rank_of(core)
+    if rank is None:
+        return
+    sem = T.sem
+    V, S, PE, Y = g.vector, g.scalar, g.tensor, g.sync
+    n_ranks = len(T.cores)
+    peers = [(rank + s) % n_ranks for s in range(1, n_ranks)]
+
+    order = sorted(range(1, n_ranks), key=lambda s: topo.die(T.cores[(rank + s) % n_ranks]) == topo.die(core))
+    dests = []
+    for n, s in enumerate(order):
+        c = T.cores[(rank + s) % n_ranks]
+        e = topo.engines(core, c)
+        e = (e[0::2] + e[1::2])[EPD * n:EPD * n + EPD]
+        rid, pid, _se = topo.addr(c)
+        dests.append((s, DstId(rid=rid, pnc=pid), sum(1 << x for x in e)))
+
+    for a in range(4):
+        Y.dma_start(T.X[32 * a:32 * a + 32, :], T.pts[a % 3::3, :]).then_inc(sem.xld, 16)
+    Y.dma_start(T.X2[0:64, :], T.nodes[6::16, :]).then_inc(sem.x2ld, 16)
+    Y.dma_start(T.X2[64:128, :], T.nodes[7::16, :]).then_inc(sem.x2ld, 16)
+    Y.dma_start(T.N0[:, :], T.nodes[:, 0:2]).then_inc(sem.n0, 16)
+    Y.wait_ge(sem.fill, 1)
+    for a in range(6):
+        Y.dma_start(T.PR[a::16, 0:384], T.pts[a % 3::3, :]).then_inc(sem.own, 16)
+    w = M // WC
+
+    def load(c):
+        Y.wait_ge(sem["fw%d" % c], 1)
+        for a in range(6):
+            Y.dma_start(T.W[a::16, w * c:w * c + w], T.nodes[a::16, w * c:w * c + w]).then_inc(sem["wl%d" % c], 16)
+
+    Y.wait_ge(sem.go, 1)
+    load(0)
+    Y.wait_ge(sem.fp, 1)
+    for s, r in enumerate(peers):
+        Y.wait_ge(sem["pa%d" % r], EPD)
+        for a in range(6):
+            Y.dma_start(T.PR[a::16, 384 * (s + 1):384 * (s + 2)],
+                        T["D%d" % r][32 * (a % 3):32 * (a % 3) + 32, :]).then_inc(sem["pl%d" % r], 16)
+    load(1)
+    load(2)
+
+    g.iota(T.KI[:, 0:1], [[1, 1]], 0, 1).then_inc(sem.iot, 1)
+    g.iota(T.CI[:, :], [[1, 128]], 0, 0).then_inc(sem.iot, 1)
+    g.iota(T.PR[:, 0:384], [[0, 384]], 0, 0).then_inc(sem.fill, 1)
+    g.wait_ge(sem.xld, 64)
+    g.remote_dma_fused([RemoteDMATransfer(dst_ids=[d], dma_engine_mask=m, remote_sem=sem["pa%d" % rank],
+                                          src=T.X[:, :], dst=T["D%d" % rank][:, :]) for s, d, m in dests],
+                       local_sem=sem.psent)
+    g.sem_inc(sem.go, 1)
+    g.iota(T.CM[:, :], [[0, 4], [1, 32]], 1, 0, allow_small_or_imprecise_dtypes=True).then_inc(sem.iot, 1)
+    g.iota(T.CQ[:, :], [[1, 4], [0, 32]], 0, 0, allow_small_or_imprecise_dtypes=True).then_inc(sem.iot, 1)
+    g.iota(T.PR[:, 384:1536], [[0, 1152]], 0, 0).then_inc(sem.fp, 1)
+    for c in range(2, WC):
+        g.iota(T.W[:, w * c:w * c + w], [[0, w]], 0, 0).then_inc(sem["fw%d" % c], 1)
+
+    nv = [0]
+
+    def v(ins):
+        nv[0] += 1
+        ins.then_inc(sem.v, 1)
+
+    def vsync():
+        V.wait_ge(sem.v, nv[0])
+
+    KF = T.KF
+
+    def col(j):
+        return KF[:, j:j + 1]
+
+    v(V.memset(T.Z[:, :], 0.0))
+    v(V.memset(KF[:, :], 0.0))
+    v(V.memset(T.KV[:, :], 0.0))
+    V.wait_ge(sem.iot, 2)
+    v(V.tensor_scalar(T.KI[:, 1:2], T.KI[:, 0:1], 15, None, OP.bitwise_and))
+    v(V.tensor_scalar(T.KI[:, 2:3], T.KI[:, 0:1], 4, None, OP.arith_shift_right))
+    v(V.tensor_scalar(T.KI[:, 3:4], T.KI[:, 0:1], 3, None, OP.bitwise_and))
+    v(V.tensor_scalar(T.KI[:, 4:5], T.KI[:, 0:1], 2, None, OP.arith_shift_right))
+    v(V.tensor_scalar(T.KI[:, 5:6], T.KI[:, 0:1], 7, None, OP.bitwise_and))
+    vsync()
+    v(V.tensor_copy(KF[:, 0:6], T.KI[:, 0:6]))
+    vsync()
+    base = nv[0]
+    p_, r_, g_, i_, k_ = [col(j) for j in range(5)]
+    v(V.tensor_scalar(col(14), r_, 14.0, None, OP.is_equal))
+    vsync()
+    V.tensor_scalar(T.Z[:, :], T.Z[:, :], col(14), None, OP.add).then_inc(sem.fz, 1)
+    V.memset(T.W[:, 0:w], 0).then_inc(sem.fw0, 1)
+
+    V.wait_ge(sem.x2ld, 32)
+    v(V.tensor_copy(T.HI[:, :], T.X2[:, :]))
+    vsync()
+    v(V.tensor_tensor(T.LO[:, :], T.X2[:, :], T.HI[:, :], OP.subtract))
+    hilo = nv[0]
+    V.memset(T.W[:, w:2 * w], 0).then_inc(sem.fw1, 1)
+    v(V.memset(T.W2[:, M:WIN2], 1.0))
+    v(V.memset(T.W[:, M:WIN], 0))
+
+    v(V.tensor_scalar(T.CJ[:, :], T.CI[:, :], 2, 3, OP.arith_shift_right, OP.bitwise_and))
+    v(V.tensor_scalar(T.CG[:, :], T.CI[:, 0:32], 2, None, OP.arith_shift_right))
+    v(V.tensor_scalar(T.CH[:, :], T.CI[:, 0:32], 7, None, OP.bitwise_and))
+    v(V.tensor_scalar(col(7), r_, 3.0, 2.0, OP.is_lt, OP.mult))
+    v(V.tensor_scalar(col(8), r_, 6.0, None, OP.is_lt))
+    v(V.tensor_scalar(col(25), r_, 12.0, 3.0, OP.is_equal, OP.mult))
+    v(V.tensor_scalar(col(55), r_, 15.0, 3.0, OP.is_equal, OP.mult))
+    for at, terms in ((16, [(6, 1.0), (8, 1.0), (14, -2048.0), (12, 4096.0), (13, -2.0)]),
+                      (30, [(10, -32.0), (11, -1.0)]),
+                      (37, [(14, -1.0), (15, 1.0)])):
+        for n, (row, c) in enumerate(terms):
+            v(V.tensor_scalar(col(at + n), r_, float(row), c, OP.is_equal, OP.mult))
+    v(V.tensor_scalar(col(34), r_, -1.0, 9.0, OP.mult, OP.add))
+    v(V.tensor_scalar(col(35), r_, 6.0, None, OP.is_ge))
+    v(V.tensor_scalar(col(39), r_, 3.0, -1.0, OP.is_ge, OP.mult))
+    v(V.tensor_scalar(col(22), r_, 7.0, None, OP.is_equal))
+    v(V.tensor_scalar(col(23), r_, 9.0, None, OP.is_equal))
+    v(V.tensor_scalar(col(24), r_, 12.0, None, OP.is_equal))
+    vsync()
+    v(V.tensor_tensor(col(36), col(34), col(35), OP.mult))
+    v(V.tensor_tensor(col(9), col(7), col(8), OP.subtract))
+    v(V.tensor_reduce(col(10), KF[:, 16:21], AxisListType.X, OP.add))
+    v(V.tensor_reduce(col(40), KF[:, 16:19], AxisListType.X, OP.add))
+    v(V.tensor_tensor(col(41), col(30), col(31), OP.add))
+    v(V.tensor_tensor(col(11), col(22), col(24), OP.subtract))
+    v(V.tensor_tensor(col(12), col(23), col(24), OP.subtract))
+    v(V.tensor_scalar(T.B32[:, :], T.CG[:, :], g_, None, OP.is_equal))
+    v(V.tensor_scalar(T.B8[:, :], T.CH[:, :], g_, None, OP.is_equal))
+    vsync()
+    v(V.tensor_tensor(col(15), col(36), col(39), OP.add))
+    v(V.tensor_tensor(col(13), col(9), col(25), OP.add))
+    v(V.tensor_tensor(col(56), col(9), col(55), OP.add))
+    v(V.tensor_tensor(col(21), col(40), col(41), OP.add))
+    v(V.tensor_scalar(col(26), col(11), -1.0, None, OP.mult))
+    v(V.tensor_scalar(col(27), col(12), -1.0, None, OP.mult))
+    v(V.tensor_scalar(col(54), col(38), -1.0, None, OP.mult))
+    vsync()
+    v(V.tensor_scalar(col(28), col(13), 8192.0, None, OP.mult))
+    v(V.tensor_scalar(col(29), col(13), -BIG, None, OP.mult))
+    v(V.tensor_scalar(col(57), col(56), -8192.0, None, OP.mult))
+    vsync()
+    half = nv[0]
+    v(V.tensor_tensor(col(58), col(57), col(20), OP.add))
+    V.wait_ge(sem.n0, 16)
+    for n in range(2):
+        v(V.tensor_tensor(col(42 + n), T.N0[:, n:n + 1], col(8), OP.mult))
+    V.wait_ge(sem.kv, 64)
+    v(V.tensor_tensor(col(52), T.KV[:, 1:2], col(18), OP.add))
+    for n, c in enumerate((14, 38, 37, 54)):
+        v(V.tensor_scalar(KF[:, 44 + 2 * n:46 + 2 * n], T.KV[:, 2:4], col(c), col(29), OP.mult, OP.add))
+    vsync()
+    v(V.tensor_tensor(col(53), col(52), col(58), OP.add))
+    cols = nv[0]
+    v(V.tensor_scalar(T.MASK[:, :], T.CJ[:, :], i_, None, OP.is_equal))
+    v(V.tensor_scalar(T.IDF[:, :], T.CI[:, :], p_, None, OP.is_equal))
+    v(V.tensor_scalar(T.SEL[:, :], T.CI[:, 0:32], k_, None, OP.is_equal))
+    v(V.tensor_scalar(T.NSEL[:, :], T.CI[:, 0:32], k_, -1.0, OP.is_equal, OP.mult))
+    vsync()
+    v(V.tensor_scalar(T.FIT[:, 0:128], T.MASK[:, :], -2.0 * TOP, TOP, OP.mult, OP.add))
+    v(V.tensor_scalar(T.FIT[:, 128:256], T.MASK[:, :], -TOP - 2048.0, TOP, OP.mult, OP.add))
+    statics = nv[0]
+
+    S.wait_ge(sem.fz, 1)
+    for c in range(3):
+        S.activation(T.W2[:, c * 512:c * 512 + 512], T.Z[:, :], FN.Copy).then_inc(sem.f2, 1)
+    S.wait_ge(sem.v, hilo)
+    for row, c, src in ((12, 0, T.HI[0:64:8, 0:2]), (13, 0, T.LO[0:64:8, 0:2]),
+                        (14, 2, T.HI[64:128:8, 0:2]), (15, 2, T.LO[64:128:8, 0:2])):
+        S.dma_start(T.KV[row::16, c:c + 2], src).then_inc(sem.kv, 16)
+    S.wait_ge(sem.v, base)
+    S.wait_ge(sem.iot, 4)
+    for u in range(4):
+        S.activation(T.KB[0:64, u:u + 1], KF[0:64, 5:6], FN.Copy, bias=4.0 * u, scale=16.0).then_inc(sem.nb, 1)
+        S.activation(T.NLB[0:64, 128 * u:128 * u + 128], T.CM[0:64, :], FN.Copy).then_inc(sem.nb, 1)
+    S.wait_ge(sem.nb, 8)
+    for u in range(4):
+        S.activation(T.NHB[0:64, 128 * u:128 * u + 128], T.CQ[0:64, :], FN.Identity, bias=T.KB[0:64, u:u + 1]
+                     ).then_inc(sem.nb, 1)
+    for c in range(3, 8):
+        S.activation(T.W2[:, c * 512:c * 512 + 512], T.Z[:, :], FN.Copy).then_inc(sem.f2, 1)
+    nr = {"rr": 0, "rs": 0}
+
+    def scaled(name, out, mask, c):
+        nr[name] += 1
+        S.activation(out, mask, FN.Copy, scale=1.0 if c is None else col(c)).then_inc(sem[name], 1)
+
+    S.wait_ge(sem.v, half)
+    scaled("rr", T.R0[:, 0:32], T.B32[:, :], 28)
+    scaled("rr", T.R0[:, 32:64], T.B32[:, :], 57)
+    scaled("rr", T.R0[:, 64:96], T.B8[:, :], 29)
+    S.wait_ge(sem.v, cols)
+    for n in range(4):
+        scaled("rr", T.R0[:, 96 + 8 * n:104 + 8 * n], T.B8[:, 0:8], 44 + 2 * n)
+        scaled("rr", T.R1[:, 64 + 8 * n:72 + 8 * n], T.B8[:, 0:8], 45 + 2 * n)
+    scaled("rr", T.R1[:, 0:32], T.B32[:, :], 52)
+    scaled("rr", T.R1[:, 32:64], T.B32[:, :], 53)
+    S.wait_ge(sem.v, statics)
+    scaled("rs", T.ID[:, :], T.IDF[:, :], None)
+    nr["rs"] += 1
+    S.activation(T.NID[:, :], T.IDF[:, :], FN.Copy, scale=-1.0).then_inc(sem.rs, 1)
+    scaled("rs", T.RA[:, 0:32], T.B32[:, :], 10)
+    scaled("rs", T.RA[:, 32:64], T.B32[:, :], 21)
+    for n, c in enumerate((11, 12, 26, 27)):
+        scaled("rs", T.RA[:, 64 + 8 * n:72 + 8 * n], T.B8[:, 0:8], c)
+    scaled("rs", T.RB[:, 0:32], T.B32[:, :], 57)
+    scaled("rs", T.RB[:, 32:64], T.B8[:, :], 29)
+
+    Y.wait_ge(sem.nb, 12)
+    Y.wait_ge(sem.f2, 8)
+    Y.wait_ge(sem.v, hilo)
+    for row, src in ((6, T.HI[0:64, :]), (7, T.HI[64:128, :]), (8, T.LO[0:64, :]), (9, T.LO[64:128, :]),
+                     (11, T.NLB[0:64, :]), (10, T.NHB[0:64, :])):
+        Y.dma_start(T.W2[row::16, 0:M], src).then_inc(sem.w2ld, 16)
+    load(3)
+
+    for s in range(n_ranks):
+        if s == 0:
+            V.wait_ge(sem.own, 96)
+        else:
+            V.wait_ge(sem["pl%d" % peers[s - 1]], 96)
+        v(V.tensor_scalar(T.P[:, s::4], T.PR[:, 384 * s:384 * s + 384], col(15), None, OP.add))
+    vsync()
+
+    PE.wait_ge(sem.v, statics)
+    PE.wait_ge(sem.rr, nr["rr"])
+
+    def gather(x):
+        t, b = divmod(x, NB)
+        B = str(b)
+        points = T.P[:, NL * b:NL * b + NL]
+        bank = T["BK" + B]
+        C, G = T["C" + B], T["G" + B]
+        if t == 0:
+            V.tensor_scalar(G[:, :], points, col(42), None, OP.is_lt).then_inc(sem["cc" + B], 1)
+            V.tensor_scalar(C[:, :], points, col(43), None, OP.is_lt).then_inc(sem["cc" + B], 1)
+            PE.wait_ge(sem["cc" + B], 1)
+            for i in range(4):
+                PE.matmul(bank[:, i:512:4], G[:, i::4], T.R0[:, :], i == 0, False).then_inc(sem["mm" + B], 1)
+            PE.wait_ge(sem["cc" + B], 2)
+            for i in range(4):
+                PE.matmul(bank[:, i:384:4], C[:, i::4], T.R1[:, :], False, i == 3).then_inc(sem["mm" + B], 1)
+            return
+        if x == NB:
+            for c in range(WC):
+                V.wait_ge(sem["wl%d" % c], 96)
+            S.wait_ge(sem.w2ld, 96)
+        V.wait_ge(sem["cu" + B], t)
+        V.tensor_tensor(C[:, :], T.W[:, 0:WIN].indirect(T["CU" + B][:, :]), points, OP.is_gt).then_inc(sem["cc" + B], 1)
+        S.wait_ge(sem["cu" + B], t)
+        S.activation(G[:, :], T.W2[:, 0:WIN2].indirect(T["CU" + B][:, :]), FN.Copy).then_inc(sem["gg" + B], 1)
+        if x == NB:
+            PE.wait_ge(sem.rs, nr["rs"])
+        PE.wait_ge(sem["gg" + B], t)
+        for i in range(4):
+            PE.matmul(bank[:, i:384:4], G[:, i::4], T.RA[:, :], i == 0, False).then_inc(sem["mm" + B], 1)
+        PE.wait_ge(sem["cc" + B], t + 2)
+        for i in range(4):
+            PE.matmul(bank[:, 128 + i:384:4], C[:, i::4], T.RB[:, :], False, i == 3).then_inc(sem["mm" + B], 1)
+
+    def move(x):
+        t, b = divmod(x, NB)
+        B = str(b)
+        if t == STEPS - 1:
+            return
+        V.wait_ge(sem["mm" + B], 8 * (t + 1))
+        V.tensor_tensor(T["IN" + B][:, :], T["BK" + B][:, 0:256], T.FIT[:, :], OP.max).then_inc(sem["mn" + B], 1)
+        PE.wait_ge(sem["mn" + B], t + 1)
+        PE.matmul(T["CP" + B][:, 0:32], T["IN" + B][:, 0:128], T.SEL[:, :], True, False).then_inc(sem["ee" + B], 1)
+        PE.matmul(T["CP" + B][:, 0:32], T["IN" + B][:, 128:256], T.NSEL[:, :], False, True).then_inc(sem["ee" + B], 1)
+
+    def cast(x):
+        t, b = divmod(x, NB)
+        B = str(b)
+        if t == STEPS - 1:
+            return
+        V.wait_ge(sem["ee" + B], 2 * t + 2)
+        V.tensor_scalar(T["CU" + B][:, :], T["CP" + B][:, 0:32], float(M), None, OP.min).then_inc(sem["cu" + B], 1)
+
+    def acc(b):
+        return T.AC1[:, 0:64] if b == NB - 1 else T.AC0[:, 64 * b:64 * b + 64]
+
+    def weigh(x):
+        t, b = divmod(x, NB)
+        B = str(b)
+        if t == STEPS - 1:
+            S.wait_ge(sem["mm" + B], 8 * (t + 1))
+        else:
+            S.wait_ge(sem["mn" + B], t + 1)
+        if t:
+            S.wait_ge(sem["ac" + B], 2 + 2 * t)
+        todo = [T["HW" + B]]
+        S.activation(T["HW" + B][:, :], T["BK" + B][:, 256:384], FN.Relu).then_inc(sem["hw" + B], 1)
+        if t == 0:
+            todo.append(T["HX" + B])
+            S.activation(T["HX" + B][:, :], T["BK" + B][:, 384:512], FN.Relu).then_inc(sem["hw" + B], 1)
+        if x == 0:
+            PE.wait_ge(sem.rs, nr["rs"])
+        PE.wait_ge(sem["hw" + B], t + 2)
+        for n, h in enumerate(todo):
+            PE.matmul(acc(b), T.ID[:, :], h[:, 0:64], t == 0 and n == 0 and b != 1, False).then_inc(sem["ac" + B], 1)
+            PE.matmul(acc(b), T.NID[:, :], h[:, 64:128], False, t == STEPS - 1 and b != 0).then_inc(sem["ac" + B], 1)
+
+    total = NB * STEPS
+    for x in range(total + 2):
+        if 0 <= x - 2 < total and x >= total:
+            cast(x - 2)
+        if x < total:
+            gather(x)
+            if 0 <= x - 2:
+                cast(x - 2)
+        if 0 <= x - 1 < total:
+            move(x - 1)
+        if 0 <= x - 2 < total:
+            weigh(x - 2)
+
+    for b in range(NB):
+        for bb in ([0, 1] if b < NB - 1 else [2]):
+            S.wait_ge(sem["ac%d" % bb], 2 + 2 * STEPS)
+            V.wait_ge(sem["ac%d" % bb], 2 + 2 * STEPS)
+        S.activation(T.TMP[:, 32 * b:32 * b + 32], acc(b)[:, 32:64], FN.Copy).then_inc(sem.lo, 1)
+        V.wait_ge(sem.lo, max(b + 1, 2))
+        for s in range(n_ranks):
+            V.tensor_tensor(T.OUT[:, 24 * s + 8 * b:24 * s + 8 * b + 8], acc(b)[:, s:32:4],
+                            T.TMP[:, 32 * b + s:32 * b + 32:4], OP.add).then_inc(sem.oa, 1)
+    g.wait_ge(sem.oa, NB * n_ranks)
+    g.remote_dma_fused([RemoteDMATransfer(dst_ids=[d], dma_engine_mask=m, remote_sem=sem["ra%d" % rank],
+                                          src=T.OUT[:, 24 * s:24 * s + 24], dst=T["L%d" % rank][:, :])
+                        for s, d, m in dests], local_sem=sem.rsent)
+    V.wait_ge(sem.oa, NB * n_ranks)
+    prev = T.OUT[:, 0:24]
+    for n, r in enumerate(peers):
+        V.wait_ge(sem["ra%d" % r], EPD)
+        if n:
+            V.wait_ge(sem.fin, n)
+        V.tensor_tensor(T.SUM[:, :], prev, T["L%d" % r][:, :], OP.add).then_inc(sem.fin, 1)
+        prev = T.SUM[:, :]
+    PE.wait_ge(sem.fin, 3)
+    PE.matmul(T.BK0[0:24, 0:128], T.SUM[:, :], T.IDF[:, :], True, True).then_inc(sem.fq, 1)
+    V.wait_ge(sem.fq, 1)
+    V.tensor_copy(T.YS[0:24, :], T.BK0[0:24, 0:128]).then_inc(sem.hl, 1)
+    for b, q in enumerate((Y, S, Y)):
+        q.wait_ge(sem.hl, 1)
+        q.dma_start(T.y[:, 128 * b:128 * b + 128], T.YS[8 * b:8 * b + 8, :]).then_inc(sem.yd, 16)
+    Y.wait_ge(sem.yd, 48)
+    g.wait_ge(sem.psent, 3 * EPD)
+    g.wait_ge(sem.rsent, 3 * EPD)

@@ -3,80 +3,80 @@ from concourse.mybir import dt, AluOpType, AxisListType, ActivationFunctionType
 
 OP = AluOpType
 FN = ActivationFunctionType
-NB = 3
-NL = 512
+NB = 4
+NL = 384
+NQ = NL // 4
+NC = NL // 16
 STEPS = 15
 M = 4096
 WIN = 4104
-WIN2 = 4112
 WC = 4
+CUT = 16
+TAIL = 1
 EPD = 4
-BIG = 262144.0
-TOP = 57344.0
+BIG = 8192.0
 
 SCRATCH = {
     "W": ("sbuf", [128, WIN], "int32"),
-    "W2": ("sbuf", [128, WIN2], "bfloat16"),
-    "Z": ("sbuf", [128, 512], "bfloat16"),
-    "X": ("dram", [128, 96], "int32"),
-    "N0": ("sbuf", [128, 2], "int32"),
-    "KV": ("sbuf", [128, 4], "bfloat16"),
-    "P": ("sbuf", [128, NB * NL], "int32"),
-    "CM": ("sbuf", [128, 128], "float32"),
-    "CQ": ("sbuf", [128, 128], "float32"),
-    "X2": ("sbuf", [128, 512], "int32"),
-    "HI": ("sbuf", [128, 512], "bfloat16"),
-    "LO": ("sbuf", [128, 512], "bfloat16"),
-    "NHB": ("sbuf", [128, 512], "bfloat16"),
-    "NLB": ("sbuf", [128, 512], "bfloat16"),
-    "PR": ("sbuf", [128, 4 * 384], "int32"),
+    "XI": ("sbuf", [128, 96], "int32"),
+    "XF": ("sbuf", [128, 96], "float32"),
+    "XW": ("sbuf", [128, 256], "int32"),
+    "HI": ("sbuf", [128, 256], "int32"),
+    "LO": ("sbuf", [128, 256], "int32"),
+    "XN": ("sbuf", [128, 256], "int32"),
+    "NP": ("sbuf", [128, 256], "int32"),
+    "NN": ("sbuf", [128, 12], "int32"),
+    "NH": ("sbuf", [128, 4], "int32"),
+    "P": ("sbuf", [128, NB * NL], "float32"),
+    "KI": ("sbuf", [128, 4], "int32"),
     "CI": ("sbuf", [128, 128], "int32"),
-    "CJ": ("sbuf", [128, 128], "int32"),
-    "CG": ("sbuf", [128, 32], "int32"),
     "CH": ("sbuf", [128, 32], "int32"),
-    "KI": ("sbuf", [128, 16], "int32"),
-    "KB": ("sbuf", [128, 8], "float32"),
+    "SI": ("sbuf", [128, 8, 16], "int32"),
+    "SP": ("sbuf", [128, 32, 16], "float32"),
     "KF": ("sbuf", [128, 64], "float32"),
-    "ID": ("sbuf", [128, 128], "bfloat16"),
-    "NID": ("sbuf", [128, 128], "bfloat16"),
-    "IDF": ("sbuf", [128, 128], "float32"),
-    "MASK": ("sbuf", [128, 128], "float32"),
-    "FIT": ("sbuf", [128, 256], "float32"),
-    "B32": ("sbuf", [128, 32], "float32"),
+    "OH": ("sbuf", [128, 16], "float32"),
     "B8": ("sbuf", [128, 32], "float32"),
-    "SEL": ("sbuf", [128, 32], "float16"),
-    "NSEL": ("sbuf", [128, 32], "float16"),
-    "RA": ("sbuf", [128, 96], "bfloat16"),
-    "RB": ("sbuf", [128, 64], "bfloat16"),
-    "R0": ("sbuf", [128, 128], "bfloat16"),
-    "R1": ("sbuf", [128, 96], "bfloat16"),
+    "IDF": ("sbuf", [128, 128], "float32"),
+    "SEL": ("sbuf", [128, 96], "float16"),
+    "S64": ("sbuf", [128, 96], "float16"),
+    "NS64": ("sbuf", [128, 96], "float16"),
+    "RA": ("sbuf", [128, 40], "float16"),
+    "RB": ("sbuf", [128, 40], "float16"),
+    "R0": ("sbuf", [128, 64], "float16"),
+    "NSEL": ("sbuf", [128, 96], "float16"),
     "OUT": ("sbuf", [128, 96], "float32"),
-    "TMP": ("sbuf", [128, 96], "float32"),
-    "SUM": ("sbuf", [128, 24], "float32"),
-    "YS": ("sbuf", [128, 128], "float32"),
-    "AC0": ("psum", [128, 512], "float32"),
-    "AC1": ("psum", [128, 512], "float32"),
+    "OW": ("sbuf", [128, 32], "float32"),
+    "YS": ("sbuf", [128, 96], "float32"),
+    "CP": ("psum", [128, 64, 8], "float32"),
+    "RL": ("psum", [128, 64, 8], "float32"),
+    "AC0": ("psum", [128, 64, 8], "float32"),
+    "AC1": ("psum", [128, 64, 8], "float32"),
 }
 for _b in range(NB):
-    SCRATCH["C%d" % _b] = ("sbuf", [128, NL], "bfloat16")
-    SCRATCH["G%d" % _b] = ("sbuf", [128, NL], "bfloat16")
-    SCRATCH["CU%d" % _b] = ("sbuf", [128, 32], "uint16")
-    SCRATCH["IN%d" % _b] = ("sbuf", [128, 256], "float16")
-    SCRATCH["HW%d" % _b] = ("sbuf", [128, 128], "bfloat16")
-    SCRATCH["HX%d" % _b] = ("sbuf", [128, 128], "bfloat16")
-    SCRATCH["BK%d" % _b] = ("psum", [128, 512], "float32")
-    SCRATCH["CP%d" % _b] = ("psum", [128, 512], "float32")
-for _r in range(4):
-    SCRATCH["D%d" % _r] = ("dram", [128, 96], "int32")
-    SCRATCH["L%d" % _r] = ("sbuf", [128, 24], "float32")
+    SCRATCH["C%d" % _b] = ("sbuf", [128, NL], "float16")
+    SCRATCH["G%d" % _b] = ("sbuf", [128, NL], "float16")
+    SCRATCH["CU%d" % _b] = ("sbuf", [128, NC], "uint16")
+    SCRATCH["IN%d" % _b] = ("sbuf", [128, 36, 8], "float16")
+    SCRATCH["HW%d" % _b] = ("sbuf", [128, 192], "float16")
+    SCRATCH["BK%d" % _b] = ("psum", [128, 64, 8], "float32")
+    SCRATCH["XR%d" % _b] = ("sbuf", [128, 96], "float32")
+    SCRATCH["L%d" % _b] = ("sbuf", [128, 32], "float32")
 
-SEMAPHORES = ["xld", "x2ld", "fill", "fz", "f2", "fp", "v", "iot", "w2ld", "own", "psent", "rsent",
-              "lo", "oa", "fin", "fq", "yd", "hl", "n0", "nb", "go", "kv", "rr", "rs"]
-SEMAPHORES += ["fw%d" % c for c in range(WC)] + ["wl%d" % c for c in range(WC)]
+SEMAPHORES = ["xld", "xwld", "nld", "wld", "xf", "v", "iot", "rs", "pc", "psent", "rsent", "oa", "ow", "fq", "hl", "yd"]
+SEMAPHORES += ["fw%d" % c for c in range(WC)]
 for _b in range(NB):
-    SEMAPHORES += ["%s%d" % (n, _b) for n in ("cu", "cc", "gg", "mm", "mn", "ee", "hw", "ac")]
-for _r in range(4):
-    SEMAPHORES += ["pa%d" % _r, "pl%d" % _r, "ra%d" % _r]
+    SEMAPHORES += ["%s%d" % (n, _b) for n in ("rl", "cu", "cc", "gg", "mm", "mn", "ee", "hw", "ac", "pa", "ra")]
+
+
+def slots():
+    out = [(0, 0), (1, 0), (0, 1), (2, 0), (3, 0)]
+    own = 2
+    for t in range(1, STEPS):
+        out += [(b, t) for b in range(1, NB)]
+        if own < STEPS - TAIL and t < STEPS - 1:
+            out.append((0, own))
+            own += 1
+    return out + [(0, t) for t in range(own, STEPS)]
 
 
 def rank_program(g, core, T, topo):
@@ -86,342 +86,344 @@ def rank_program(g, core, T, topo):
     sem = T.sem
     V, S, PE, Y = g.vector, g.scalar, g.tensor, g.sync
     n_ranks = len(T.cores)
-    peers = [(rank + s) % n_ranks for s in range(1, n_ranks)]
+    src = [(rank + s) % n_ranks for s in range(n_ranks)]
+    count = {}
 
-    order = sorted(range(1, n_ranks), key=lambda s: topo.die(T.cores[(rank + s) % n_ranks]) == topo.die(core))
+    def inc(ins, name, n=1):
+        ins.then_inc(sem[name], n)
+        count[name] = count.get(name, 0) + n
+        return count[name]
+
+    def wait(q, name, n=None):
+        q.wait_ge(sem[name], count[name] if n is None else n)
+
+    order = sorted(range(1, n_ranks), key=lambda s: topo.die(T.cores[src[s]]) == topo.die(core))
     dests = []
     for n, s in enumerate(order):
-        c = T.cores[(rank + s) % n_ranks]
+        c = T.cores[src[s]]
         e = topo.engines(core, c)
         e = (e[0::2] + e[1::2])[EPD * n:EPD * n + EPD]
         rid, pid, _se = topo.addr(c)
         dests.append((s, DstId(rid=rid, pnc=pid), sum(1 << x for x in e)))
 
-    for a in range(4):
-        Y.dma_start(T.X[32 * a:32 * a + 32, :], T.pts[a % 3::3, :]).then_inc(sem.xld, 16)
-    Y.dma_start(T.X2[0:64, :], T.nodes[6::16, :]).then_inc(sem.x2ld, 16)
-    Y.dma_start(T.X2[64:128, :], T.nodes[7::16, :]).then_inc(sem.x2ld, 16)
-    Y.dma_start(T.N0[:, :], T.nodes[:, 0:2]).then_inc(sem.n0, 16)
-    Y.wait_ge(sem.fill, 1)
-    for a in range(6):
-        Y.dma_start(T.PR[a::16, 0:384], T.pts[a % 3::3, :]).then_inc(sem.own, 16)
     w = M // WC
-
-    def load(c):
-        Y.wait_ge(sem["fw%d" % c], 1)
-        for a in range(6):
-            Y.dma_start(T.W[a::16, w * c:w * c + w], T.nodes[a::16, w * c:w * c + w]).then_inc(sem["wl%d" % c], 16)
-
-    Y.wait_ge(sem.go, 1)
-    load(0)
-    Y.wait_ge(sem.fp, 1)
-    for s, r in enumerate(peers):
-        Y.wait_ge(sem["pa%d" % r], EPD)
-        for a in range(6):
-            Y.dma_start(T.PR[a::16, 384 * (s + 1):384 * (s + 2)],
-                        T["D%d" % r][32 * (a % 3):32 * (a % 3) + 32, :]).then_inc(sem["pl%d" % r], 16)
-    load(1)
-    load(2)
-
-    g.iota(T.KI[:, 0:1], [[1, 1]], 0, 1).then_inc(sem.iot, 1)
-    g.iota(T.CI[:, :], [[1, 128]], 0, 0).then_inc(sem.iot, 1)
-    g.iota(T.PR[:, 0:384], [[0, 384]], 0, 0).then_inc(sem.fill, 1)
-    g.wait_ge(sem.xld, 64)
-    g.remote_dma_fused([RemoteDMATransfer(dst_ids=[d], dma_engine_mask=m, remote_sem=sem["pa%d" % rank],
-                                          src=T.X[:, :], dst=T["D%d" % rank][:, :]) for s, d, m in dests],
-                       local_sem=sem.psent)
-    g.sem_inc(sem.go, 1)
-    g.iota(T.CM[:, :], [[0, 4], [1, 32]], 1, 0, allow_small_or_imprecise_dtypes=True).then_inc(sem.iot, 1)
-    g.iota(T.CQ[:, :], [[1, 4], [0, 32]], 0, 0, allow_small_or_imprecise_dtypes=True).then_inc(sem.iot, 1)
-    g.iota(T.PR[:, 384:1536], [[0, 1152]], 0, 0).then_inc(sem.fp, 1)
-    for c in range(2, WC):
-        g.iota(T.W[:, w * c:w * c + w], [[0, w]], 0, 0).then_inc(sem["fw%d" % c], 1)
-
-    nv = [0]
-
-    def v(ins):
-        nv[0] += 1
-        ins.then_inc(sem.v, 1)
-
-    def vsync():
-        V.wait_ge(sem.v, nv[0])
-
-    KF = T.KF
+    KF, OH = T.KF, T.OH
 
     def col(j):
         return KF[:, j:j + 1]
 
-    v(V.memset(T.Z[:, :], 0.0))
-    v(V.memset(KF[:, :], 0.0))
-    v(V.memset(T.KV[:, :], 0.0))
-    V.wait_ge(sem.iot, 2)
+    def oh(r):
+        return OH[:, r:r + 1]
+
+    def v(ins):
+        return inc(ins, "v")
+
+    def vsync():
+        wait(V, "v")
+
+    inc(Y.dma_start(T.XI[0:96, :], T.pts[:, :]), "xld", 16)
+    inc(Y.dma_start(T.XW[:, :], T.nodes[7::16, :]), "xwld", 16)
+
+    inc(g.iota(T.KI[:, 0:1], [[1, 1]], 0, 1), "iot")
+    inc(g.iota(T.CI[:, :], [[1, 128]], 0, 0), "iot")
+    first = inc(g.iota(T.CH[:, :], [[0, 4], [1, 8]], 0, 0), "iot")
+    inc(g.iota(T.SI[:, :, 0:12], [[12, 8], [0, 4], [4, 3]], 0, -1), "iot")
+    inc(g.iota(T.SI[:, :, 12:16], [[0, 32]], 999, 0), "iot")
+    inc(g.iota(T.XN[:, :], [[1, 256]], 0, 256), "iot")
+
+    inc(V.memset(T.W[:, 0:w], 0), "fw0")
+    nn = v(V.memset(T.NN[:, :], 0))
+    v(V.memset(T.XF[96:128, :], 0.0))
+    wait(V, "iot", first)
     v(V.tensor_scalar(T.KI[:, 1:2], T.KI[:, 0:1], 15, None, OP.bitwise_and))
     v(V.tensor_scalar(T.KI[:, 2:3], T.KI[:, 0:1], 4, None, OP.arith_shift_right))
-    v(V.tensor_scalar(T.KI[:, 3:4], T.KI[:, 0:1], 3, None, OP.bitwise_and))
-    v(V.tensor_scalar(T.KI[:, 4:5], T.KI[:, 0:1], 2, None, OP.arith_shift_right))
-    v(V.tensor_scalar(T.KI[:, 5:6], T.KI[:, 0:1], 7, None, OP.bitwise_and))
+    v(V.memset(T.OUT[96:128, :], 0.0))
     vsync()
-    v(V.tensor_copy(KF[:, 0:6], T.KI[:, 0:6]))
+    v(V.tensor_copy(KF[:, 0:3], T.KI[:, 0:3]))
+    for b in range(NB):
+        v(V.memset(T["IN%d" % b][:, :, :], 0.0))
     vsync()
-    base = nv[0]
-    p_, r_, g_, i_, k_ = [col(j) for j in range(5)]
-    v(V.tensor_scalar(col(14), r_, 14.0, None, OP.is_equal))
-    vsync()
-    V.tensor_scalar(T.Z[:, :], T.Z[:, :], col(14), None, OP.add).then_inc(sem.fz, 1)
-    V.memset(T.W[:, 0:w], 0).then_inc(sem.fw0, 1)
-
-    V.wait_ge(sem.x2ld, 32)
-    v(V.tensor_copy(T.HI[:, :], T.X2[:, :]))
-    vsync()
-    v(V.tensor_tensor(T.LO[:, :], T.X2[:, :], T.HI[:, :], OP.subtract))
-    hilo = nv[0]
-    V.memset(T.W[:, w:2 * w], 0).then_inc(sem.fw1, 1)
-    v(V.memset(T.W2[:, M:WIN2], 1.0))
-    v(V.memset(T.W[:, M:WIN], 0))
-
-    v(V.tensor_scalar(T.CJ[:, :], T.CI[:, :], 2, 3, OP.arith_shift_right, OP.bitwise_and))
-    v(V.tensor_scalar(T.CG[:, :], T.CI[:, 0:32], 2, None, OP.arith_shift_right))
-    v(V.tensor_scalar(T.CH[:, :], T.CI[:, 0:32], 7, None, OP.bitwise_and))
-    v(V.tensor_scalar(col(7), r_, 3.0, 2.0, OP.is_lt, OP.mult))
-    v(V.tensor_scalar(col(8), r_, 6.0, None, OP.is_lt))
-    v(V.tensor_scalar(col(25), r_, 12.0, 3.0, OP.is_equal, OP.mult))
-    v(V.tensor_scalar(col(55), r_, 15.0, 3.0, OP.is_equal, OP.mult))
-    for at, terms in ((16, [(6, 1.0), (8, 1.0), (14, -2048.0), (12, 4096.0), (13, -2.0)]),
-                      (30, [(10, -32.0), (11, -1.0)]),
-                      (37, [(14, -1.0), (15, 1.0)])):
-        for n, (row, c) in enumerate(terms):
-            v(V.tensor_scalar(col(at + n), r_, float(row), c, OP.is_equal, OP.mult))
-    v(V.tensor_scalar(col(34), r_, -1.0, 9.0, OP.mult, OP.add))
-    v(V.tensor_scalar(col(35), r_, 6.0, None, OP.is_ge))
-    v(V.tensor_scalar(col(39), r_, 3.0, -1.0, OP.is_ge, OP.mult))
-    v(V.tensor_scalar(col(22), r_, 7.0, None, OP.is_equal))
-    v(V.tensor_scalar(col(23), r_, 9.0, None, OP.is_equal))
-    v(V.tensor_scalar(col(24), r_, 12.0, None, OP.is_equal))
-    vsync()
-    v(V.tensor_tensor(col(36), col(34), col(35), OP.mult))
-    v(V.tensor_tensor(col(9), col(7), col(8), OP.subtract))
-    v(V.tensor_reduce(col(10), KF[:, 16:21], AxisListType.X, OP.add))
-    v(V.tensor_reduce(col(40), KF[:, 16:19], AxisListType.X, OP.add))
-    v(V.tensor_tensor(col(41), col(30), col(31), OP.add))
-    v(V.tensor_tensor(col(11), col(22), col(24), OP.subtract))
-    v(V.tensor_tensor(col(12), col(23), col(24), OP.subtract))
-    v(V.tensor_scalar(T.B32[:, :], T.CG[:, :], g_, None, OP.is_equal))
+    p_, r_, g_ = col(0), col(1), col(2)
+    v(V.tensor_scalar(OH[:, :], T.CI[:, 0:16], r_, None, OP.is_equal))
+    v(V.tensor_scalar(KF[:, 4:8], T.CI[:, 3:13:3], r_, None, OP.is_gt))
     v(V.tensor_scalar(T.B8[:, :], T.CH[:, :], g_, None, OP.is_equal))
-    vsync()
-    v(V.tensor_tensor(col(15), col(36), col(39), OP.add))
-    v(V.tensor_tensor(col(13), col(9), col(25), OP.add))
-    v(V.tensor_tensor(col(56), col(9), col(55), OP.add))
-    v(V.tensor_tensor(col(21), col(40), col(41), OP.add))
-    v(V.tensor_scalar(col(26), col(11), -1.0, None, OP.mult))
-    v(V.tensor_scalar(col(27), col(12), -1.0, None, OP.mult))
-    v(V.tensor_scalar(col(54), col(38), -1.0, None, OP.mult))
-    vsync()
-    v(V.tensor_scalar(col(28), col(13), 8192.0, None, OP.mult))
-    v(V.tensor_scalar(col(29), col(13), -BIG, None, OP.mult))
-    v(V.tensor_scalar(col(57), col(56), -8192.0, None, OP.mult))
-    vsync()
-    half = nv[0]
-    v(V.tensor_tensor(col(58), col(57), col(20), OP.add))
-    V.wait_ge(sem.n0, 16)
-    for n in range(2):
-        v(V.tensor_tensor(col(42 + n), T.N0[:, n:n + 1], col(8), OP.mult))
-    V.wait_ge(sem.kv, 64)
-    v(V.tensor_tensor(col(52), T.KV[:, 1:2], col(18), OP.add))
-    for n, c in enumerate((14, 38, 37, 54)):
-        v(V.tensor_scalar(KF[:, 44 + 2 * n:46 + 2 * n], T.KV[:, 2:4], col(c), col(29), OP.mult, OP.add))
-    vsync()
-    v(V.tensor_tensor(col(53), col(52), col(58), OP.add))
-    cols = nv[0]
-    v(V.tensor_scalar(T.MASK[:, :], T.CJ[:, :], i_, None, OP.is_equal))
     v(V.tensor_scalar(T.IDF[:, :], T.CI[:, :], p_, None, OP.is_equal))
-    v(V.tensor_scalar(T.SEL[:, :], T.CI[:, 0:32], k_, None, OP.is_equal))
-    v(V.tensor_scalar(T.NSEL[:, :], T.CI[:, 0:32], k_, -1.0, OP.is_equal, OP.mult))
+    wait(V, "xld")
+    inc(V.tensor_copy(T.XF[0:96, :], T.XI[0:96, :]), "xf")
     vsync()
-    v(V.tensor_scalar(T.FIT[:, 0:128], T.MASK[:, :], -2.0 * TOP, TOP, OP.mult, OP.add))
-    v(V.tensor_scalar(T.FIT[:, 128:256], T.MASK[:, :], -TOP - 2048.0, TOP, OP.mult, OP.add))
-    statics = nv[0]
-
-    S.wait_ge(sem.fz, 1)
-    for c in range(3):
-        S.activation(T.W2[:, c * 512:c * 512 + 512], T.Z[:, :], FN.Copy).then_inc(sem.f2, 1)
-    S.wait_ge(sem.v, hilo)
-    for row, c, src in ((12, 0, T.HI[0:64:8, 0:2]), (13, 0, T.LO[0:64:8, 0:2]),
-                        (14, 2, T.HI[64:128:8, 0:2]), (15, 2, T.LO[64:128:8, 0:2])):
-        S.dma_start(T.KV[row::16, c:c + 2], src).then_inc(sem.kv, 16)
-    S.wait_ge(sem.v, base)
-    S.wait_ge(sem.iot, 4)
+    masks = count["v"]
+    lt3, lt6, lt9, lt12 = col(4), col(5), col(6), col(7)
+    v(V.tensor_scalar(col(8), lt3, 2.0, lt6, OP.mult, OP.subtract))
+    v(V.tensor_scalar(col(9), lt9, 2.0, lt12, OP.mult, OP.subtract))
+    v(V.tensor_scalar(col(10), lt12, lt6, None, OP.subtract))
+    v(V.tensor_scalar(col(11), lt12, -1.0, 1.0, OP.mult, OP.add))
+    v(V.tensor_scalar(col(12), oh(15), -3 * BIG, None, OP.mult))
+    v(V.tensor_scalar(col(13), oh(15), -6 * BIG, None, OP.mult))
+    v(V.tensor_scalar(col(14), oh(13), -1.0, None, OP.mult))
+    v(V.tensor_scalar(col(15), oh(6), oh(7), oh(8), OP.add, OP.add))
+    v(V.tensor_scalar(col(16), oh(9), -2047.0, None, OP.mult))
+    v(V.tensor_scalar(col(17), oh(6), oh(10), -2048.0, OP.add, OP.mult))
+    for n, (k, row, op) in enumerate(((13.0, 6, OP.add), (12.0, 7, OP.add), (12.0, 8, OP.add), (12.0, 7, OP.subtract))):
+        v(V.tensor_scalar(col(19 + n), oh(10), k, oh(row), OP.mult, op))
+    v(V.tensor_scalar(col(35), oh(14), -2.0, None, OP.mult))
+    v(V.memset(T.RB[:, 0:16], 0.0))
+    v(V.tensor_scalar(T.W[:, M:M + 1], lt3, 2.0 ** 22, float(M), OP.mult, OP.add))
+    vsync()
+    v(V.tensor_scalar(col(23), col(8), col(9), lt6, OP.add, OP.subtract))
+    v(V.tensor_scalar(col(24), col(8), -BIG, None, OP.mult))
+    v(V.tensor_scalar(col(18), col(19), oh(9), None, OP.subtract))
+    v(V.tensor_scalar(col(25), col(8), -BIG, col(12), OP.mult, OP.add))
+    v(V.tensor_scalar(col(26), col(15), oh(9), None, OP.add))
+    v(V.tensor_scalar(col(27), col(16), col(17), None, OP.add))
+    wait(V, "xwld")
+    v(V.tensor_scalar(T.HI[:, :], T.XW[:, :], 6, None, OP.arith_shift_right))
+    v(V.tensor_scalar(T.LO[:, :], T.XW[:, :], 63, None, OP.bitwise_and))
+    wait(V, "iot")
+    rows = v(V.tensor_scalar(T.NP[:, :], T.XN[:, :], M - 1, None, OP.bitwise_and))
     for u in range(4):
-        S.activation(T.KB[0:64, u:u + 1], KF[0:64, 5:6], FN.Copy, bias=4.0 * u, scale=16.0).then_inc(sem.nb, 1)
-        S.activation(T.NLB[0:64, 128 * u:128 * u + 128], T.CM[0:64, :], FN.Copy).then_inc(sem.nb, 1)
-    S.wait_ge(sem.nb, 8)
-    for u in range(4):
-        S.activation(T.NHB[0:64, 128 * u:128 * u + 128], T.CQ[0:64, :], FN.Identity, bias=T.KB[0:64, u:u + 1]
-                     ).then_inc(sem.nb, 1)
-    for c in range(3, 8):
-        S.activation(T.W2[:, c * 512:c * 512 + 512], T.Z[:, :], FN.Copy).then_inc(sem.f2, 1)
-    nr = {"rr": 0, "rs": 0}
+        place = v(V.tensor_scalar(T.SP[:, 8 * u:8 * u + 8, :], T.SI[:, :, :], float(-u), None, OP.is_equal))
+    wait(V, "v", rows)
+    v(V.tensor_scalar(col(28), col(23), lt12, 0.5, OP.subtract, OP.mult))
+    v(V.tensor_scalar(col(29), col(23), -BIG, col(13), OP.mult, OP.add))
 
-    def scaled(name, out, mask, c):
-        nr[name] += 1
-        S.activation(out, mask, FN.Copy, scale=1.0 if c is None else col(c)).then_inc(sem[name], 1)
+    wait(g, "xf")
+    wait(g, "v", masks)
+    g.remote_dma_fused([RemoteDMATransfer(dst_ids=[d], dma_engine_mask=m, remote_sem=sem["pa%d" % rank],
+                                          src=T.XF[:, :], dst=T["XR%d" % rank][:, :]) for s, d, m in dests],
+                       local_sem=sem.psent)
+    inc(g.iota(T.W[:, 3 * w:4 * w], [[0, w]], 0, 0), "fw3")
 
-    S.wait_ge(sem.v, half)
-    scaled("rr", T.R0[:, 0:32], T.B32[:, :], 28)
-    scaled("rr", T.R0[:, 32:64], T.B32[:, :], 57)
-    scaled("rr", T.R0[:, 64:96], T.B8[:, :], 29)
-    S.wait_ge(sem.v, cols)
-    for n in range(4):
-        scaled("rr", T.R0[:, 96 + 8 * n:104 + 8 * n], T.B8[:, 0:8], 44 + 2 * n)
-        scaled("rr", T.R1[:, 64 + 8 * n:72 + 8 * n], T.B8[:, 0:8], 45 + 2 * n)
-    scaled("rr", T.R1[:, 0:32], T.B32[:, :], 52)
-    scaled("rr", T.R1[:, 32:64], T.B32[:, :], 53)
-    S.wait_ge(sem.v, statics)
-    scaled("rs", T.ID[:, :], T.IDF[:, :], None)
-    nr["rs"] += 1
-    S.activation(T.NID[:, :], T.IDF[:, :], FN.Copy, scale=-1.0).then_inc(sem.rs, 1)
-    scaled("rs", T.RA[:, 0:32], T.B32[:, :], 10)
-    scaled("rs", T.RA[:, 32:64], T.B32[:, :], 21)
-    for n, c in enumerate((11, 12, 26, 27)):
-        scaled("rs", T.RA[:, 64 + 8 * n:72 + 8 * n], T.B8[:, 0:8], c)
-    scaled("rs", T.RB[:, 0:32], T.B32[:, :], 57)
-    scaled("rs", T.RB[:, 32:64], T.B8[:, :], 29)
+    wait(Y, "v", nn)
+    for n, shift in enumerate((0, 6, 7)):
+        inc(Y.dma_start(T.NN[shift:128, 4 * n:4 * n + 2], T.nodes[0:128 - shift, 0:2]), "nld", 16)
+    wait(S, "fw0")
+    for c in (1, 2):
+        inc(S.activation(T.W[:, w * c:w * c + w], T.W[:, 0:w], FN.Copy), "fw%d" % c)
+    wait(Y, "fw1")
+    wait(Y, "fw2")
+    for a in range(7):
+        inc(Y.dma_start(T.W[a::16, 0:3 * w], T.nodes[a::16, 0:3 * w]), "wld", 16)
+    wait(Y, "fw3")
+    for a in range(7):
+        inc(Y.dma_start(T.W[a::16, 3 * w:M], T.nodes[a::16, 3 * w:M]), "wld", 16)
+    wait(Y, "v", rows)
+    for a, t in ((7, T.HI), (8, T.LO), (9, T.NP)):
+        inc(Y.dma_start(T.W[a::16, 0:M], t[:, :]), "wld", 16)
 
-    Y.wait_ge(sem.nb, 12)
-    Y.wait_ge(sem.f2, 8)
-    Y.wait_ge(sem.v, hilo)
-    for row, src in ((6, T.HI[0:64, :]), (7, T.HI[64:128, :]), (8, T.LO[0:64, :]), (9, T.LO[64:128, :]),
-                     (11, T.NLB[0:64, :]), (10, T.NHB[0:64, :])):
-        Y.dma_start(T.W2[row::16, 0:M], src).then_inc(sem.w2ld, 16)
-    load(3)
+    wait(V, "nld")
+    v(V.tensor_scalar(T.NH[:, 0:2], T.NN[:, 4:6], 6, None, OP.arith_shift_right))
+    v(V.tensor_scalar(T.NH[:, 2:4], T.NN[:, 8:10], 63, None, OP.bitwise_and))
+    v(V.tensor_scalar(col(30), T.NN[:, 0:1], lt6, col(11), OP.mult, OP.add))
+    v(V.tensor_scalar(col(31), T.NN[:, 5:6], 2048.0, oh(12), OP.subtract, OP.mult))
+    vsync()
+    v(V.tensor_scalar(col(33), T.NN[:, 5:6], col(10), col(30), OP.mult, OP.add))
+    v(V.tensor_scalar(col(40), col(31), col(29), col(35), OP.add, OP.add))
+    v(V.tensor_scalar(col(41), col(31), col(25), None, OP.subtract))
+    for n, (node, c) in enumerate(((1, 29), (0, 25))):
+        for k, (at, row) in enumerate(((0, oh(13)), (2, oh(14)), (0, col(14)))):
+            v(V.tensor_scalar(col(42 + 3 * n + k), T.NH[:, at + node:at + node + 1], row, col(c), OP.mult, OP.add))
+    vsync()
+    cols = v(V.tensor_scalar(col(34), col(33), col(28), None, OP.subtract))
+    vsync()
 
-    for s in range(n_ranks):
-        if s == 0:
-            V.wait_ge(sem.own, 96)
+    def scaled(out, mask, c):
+        return inc(S.activation(out, mask, FN.Copy, scale=c), "rs")
+
+    wait(S, "v", masks)
+    def block(R, n):
+        return R[:, n:16:2] if n < 2 else R[:, 8 * n:8 * n + 8]
+
+    for out, c in ((T.SEL, 1.0), (T.NSEL, -1.0), (T.S64, 64.0), (T.NS64, -64.0)):
+        scaled(out[:, :], T.IDF[:, 0:96], c)
+    wait(S, "v", rows)
+    for n, c in enumerate((col(18), oh(6), col(20), col(21), col(22))):
+        scaled(block(T.RA, n), T.B8[:, 0:8], c)
+    scaled(block(T.RB, 0), T.B8[:, 0:8], col(24))
+    scaled(T.RB[:, 16:40], T.B8[:, 0:24], col(24))
+    wait(S, "v", cols)
+    for n in range(8):
+        scaled(block(T.R0, n), T.B8[:, 0:8], col(40 + n))
+
+    land = [T.RL, T.AC1, T.RL, T["BK%d" % (NB - 1)]]
+    seq = slots()
+    state = {"moved": -1, "cast": -1, "weighed": -1, "window": False}
+    copied = {}
+    last_other = max(x for x, (b, t) in enumerate(seq) if b)
+
+    shared = 1 + 2 * ((max(x for x, (b, t) in enumerate(seq) if t == 0) + 1) // 2)
+
+    def offsets(x):
+        return "RL" if x >= shared and x % 2 else "CP"
+
+    def bring(b):
+        if b == 0:
+            wait(PE, "v", place)
+            wait(PE, "xf")
         else:
-            V.wait_ge(sem["pl%d" % peers[s - 1]], 96)
-        v(V.tensor_scalar(T.P[:, s::4], T.PR[:, 384 * s:384 * s + 384], col(15), None, OP.add))
-    vsync()
+            PE.wait_ge(sem["pa%d" % src[b]], EPD)
+        if b == 2:
+            wait(PE, "pc", copied[0])
+        X = T.XF if b == 0 else T["XR%d" % src[b]]
+        for u in range(4):
+            ins = PE.matmul(land[b][:, 0:NL // 8, u::4], T.SP[0:96, 8 * u:8 * u + 8, :], X[0:96, :], u == 0, u == 3)
+        inc(ins, "rl%d" % b)
 
-    PE.wait_ge(sem.v, statics)
-    PE.wait_ge(sem.rr, nr["rr"])
-
-    def gather(x):
-        t, b = divmod(x, NB)
+    def gather(x, c0, c1):
+        b, t = seq[x]
         B = str(b)
-        points = T.P[:, NL * b:NL * b + NL]
+        C = T["C" + B]
+        if t == 0:
+            wait(V, "rl" + B)
+            points = land[b][:, 0:NL // 8, :]
+            inc(V.tensor_scalar(C[:, :], points, col(34), None, OP.is_lt), "cc" + B)
+            wait(S, "cc" + B)
+            copied[b] = inc(S.activation(T.P[:, NL * b:NL * b + NL], points, FN.Identity, bias=col(28)), "pc")
+            return
+        if c0 == 0:
+            if not state["window"]:
+                state["window"] = True
+                wait(V, "wld")
+                wait(S, "wld")
+            if t == 1:
+                wait(V, "pc", copied[b])
+            wait(V, "cu" + B)
+            wait(S, "cu" + B)
+            inc(S.activation(T["G" + B][:, :], T.W[:, 0:M + 1].indirect(T["CU" + B][:, :]), FN.Identity,
+                             bias=col(27), scale=col(26)), "gg" + B)
+        inc(V.tensor_tensor(C[:, 16 * c0:16 * c1], T.W[:, 0:M + 1].indirect(T["CU" + B][:, c0:c1]),
+                            T.P[:, NL * b + 16 * c0:NL * b + 16 * c1], OP.is_gt), "cc" + B)
+
+    def turn(x):
+        b, t = seq[x]
+        B = str(b)
         bank = T["BK" + B]
         C, G = T["C" + B], T["G" + B]
+        if x == 0:
+            wait(PE, "rs")
         if t == 0:
-            V.tensor_scalar(G[:, :], points, col(42), None, OP.is_lt).then_inc(sem["cc" + B], 1)
-            V.tensor_scalar(C[:, :], points, col(43), None, OP.is_lt).then_inc(sem["cc" + B], 1)
-            PE.wait_ge(sem["cc" + B], 1)
+            wait(PE, "cc" + B)
+            if land[b].name == bank.name:
+                wait(PE, "pc", copied[b])
             for i in range(4):
-                PE.matmul(bank[:, i:512:4], G[:, i::4], T.R0[:, :], i == 0, False).then_inc(sem["mm" + B], 1)
-            PE.wait_ge(sem["cc" + B], 2)
+                ins = PE.matmul(bank[0:NQ, 0:32, 2 * i:2 * i + 2], C[:, i::4], T.R0[:, :], i == 0, i == 3)
+        else:
+            wait(PE, "gg" + B)
             for i in range(4):
-                PE.matmul(bank[:, i:384:4], C[:, i::4], T.R1[:, :], False, i == 3).then_inc(sem["mm" + B], 1)
-            return
-        if x == NB:
-            for c in range(WC):
-                V.wait_ge(sem["wl%d" % c], 96)
-            S.wait_ge(sem.w2ld, 96)
-        V.wait_ge(sem["cu" + B], t)
-        V.tensor_tensor(C[:, :], T.W[:, 0:WIN].indirect(T["CU" + B][:, :]), points, OP.is_gt).then_inc(sem["cc" + B], 1)
-        S.wait_ge(sem["cu" + B], t)
-        S.activation(G[:, :], T.W2[:, 0:WIN2].indirect(T["CU" + B][:, :]), FN.Copy).then_inc(sem["gg" + B], 1)
-        if x == NB:
-            PE.wait_ge(sem.rs, nr["rs"])
-        PE.wait_ge(sem["gg" + B], t)
-        for i in range(4):
-            PE.matmul(bank[:, i:384:4], G[:, i::4], T.RA[:, :], i == 0, False).then_inc(sem["mm" + B], 1)
-        PE.wait_ge(sem["cc" + B], t + 2)
-        for i in range(4):
-            PE.matmul(bank[:, 128 + i:384:4], C[:, i::4], T.RB[:, :], False, i == 3).then_inc(sem["mm" + B], 1)
+                PE.matmul(bank[0:NQ, 0:20, 2 * i:2 * i + 2], G[:, i::4], T.RA[:, :], i == 0, False)
+            wait(PE, "cc" + B)
+            for i in range(4):
+                ins = PE.matmul(bank[0:NQ, 0:20, 2 * i:2 * i + 2], C[:, i::4], T.RB[:, :], False, i == 3)
+        inc(ins, "mm" + B)
 
     def move(x):
-        t, b = divmod(x, NB)
+        if x <= state["moved"]:
+            return
+        cast(x - 2)
+        state["moved"] = x
+        b, t = seq[x]
         B = str(b)
         if t == STEPS - 1:
             return
-        V.wait_ge(sem["mm" + B], 8 * (t + 1))
-        V.tensor_tensor(T["IN" + B][:, :], T["BK" + B][:, 0:256], T.FIT[:, :], OP.max).then_inc(sem["mn" + B], 1)
-        PE.wait_ge(sem["mn" + B], t + 1)
-        PE.matmul(T["CP" + B][:, 0:32], T["IN" + B][:, 0:128], T.SEL[:, :], True, False).then_inc(sem["ee" + B], 1)
-        PE.matmul(T["CP" + B][:, 0:32], T["IN" + B][:, 128:256], T.NSEL[:, :], False, True).then_inc(sem["ee" + B], 1)
+        IN = T["IN" + B]
+        wait(V, "mm" + B)
+        inc(V.tensor_scalar(IN[0:NQ, 3:35:4, :], T["BK" + B][0:NQ, 0:8, :], -2048.0, None, OP.max), "mn" + B)
+        for y in (x - 2, x - 1):
+            if y >= 0 and offsets(y) == offsets(x):
+                cast(y)
+                if seq[y][1] < STEPS - 1:
+                    wait(PE, "cu%d" % seq[y][0])
+        if x == shared:
+            wait(PE, "pc")
+        wait(PE, "mn" + B)
+        for n in range(8):
+            h, k = divmod(n, 4)
+            ins = PE.matmul(T[offsets(x)][:, 0:NC // 8, :], IN[0:NQ, 3 - k:35 - k, 1 - h::2],
+                            (T.SEL, T.NSEL)[h][0:NQ, k::4], n == 0, n == 7)
+        inc(ins, "ee" + B)
 
     def cast(x):
-        t, b = divmod(x, NB)
+        if x <= state["cast"]:
+            return
+        move(x)
+        state["cast"] = x
+        b, t = seq[x]
         B = str(b)
         if t == STEPS - 1:
             return
-        V.wait_ge(sem["ee" + B], 2 * t + 2)
-        V.tensor_scalar(T["CU" + B][:, :], T["CP" + B][:, 0:32], float(M), None, OP.min).then_inc(sem["cu" + B], 1)
+        wait(V, "ee" + B)
+        inc(V.tensor_scalar(T["CU" + B][:, :], T[offsets(x)][:, 0:NC // 8, :], float(M), None, OP.min), "cu" + B)
 
     def acc(b):
-        return T.AC1[:, 0:64] if b == NB - 1 else T.AC0[:, 64 * b:64 * b + 64]
+        return T.AC1[0:NQ, 4 * b - 4:4 * b, :] if b else T.AC0[0:NQ, 0:4, :]
 
     def weigh(x):
-        t, b = divmod(x, NB)
+        if x <= state["weighed"]:
+            return
+        weigh(x - 1)
+        move(x)
+        state["weighed"] = x
+        b, t = seq[x]
         B = str(b)
-        if t == STEPS - 1:
-            S.wait_ge(sem["mm" + B], 8 * (t + 1))
-        else:
-            S.wait_ge(sem["mn" + B], t + 1)
+        H = T["HW" + B]
+        wait(S, ("mm" if t == STEPS - 1 else "mn") + B)
         if t:
-            S.wait_ge(sem["ac" + B], 2 + 2 * t)
-        todo = [T["HW" + B]]
-        S.activation(T["HW" + B][:, :], T["BK" + B][:, 256:384], FN.Relu).then_inc(sem["hw" + B], 1)
-        if t == 0:
-            todo.append(T["HX" + B])
-            S.activation(T["HX" + B][:, :], T["BK" + B][:, 384:512], FN.Relu).then_inc(sem["hw" + B], 1)
-        if x == 0:
-            PE.wait_ge(sem.rs, nr["rs"])
-        PE.wait_ge(sem["hw" + B], t + 2)
-        for n, h in enumerate(todo):
-            PE.matmul(acc(b), T.ID[:, :], h[:, 0:64], t == 0 and n == 0 and b != 1, False).then_inc(sem["ac" + B], 1)
-            PE.matmul(acc(b), T.NID[:, :], h[:, 64:128], False, t == STEPS - 1 and b != 0).then_inc(sem["ac" + B], 1)
+            wait(S, "ac" + B)
+        n = 192 if t == 0 else 96
+        inc(S.activation(H[0:NQ, 0:n], T["BK" + B][0:NQ, 8:8 + n // 8, :], FN.Relu), "hw" + B)
+        wait(PE, "hw" + B)
+        for h in range(n // 32):
+            ins = PE.matmul(acc(b), (T.S64, T.SEL, T.NS64)[h % 3][0:NQ, :], H[0:NQ, 32 * h:32 * h + 32],
+                            t == 0 and h == 0 and b < 2, h == 2 and t == STEPS - 1 and (b == 0 or x == last_other))
+        inc(ins, "ac" + B)
+        if x == last_other:
+            for bb in range(1, NB):
+                wait(S, "ac%d" % bb)
+            inc(S.activation(T.OUT[0:NQ, :], T.AC1[0:NQ, 0:12, :], FN.Copy), "oa")
+            wait(g, "oa")
+            g.remote_dma_fused([RemoteDMATransfer(dst_ids=[d], dma_engine_mask=m, remote_sem=sem["ra%d" % rank],
+                                                  src=T.OUT[:, 32 * s - 32:32 * s], dst=T["L%d" % rank][:, :])
+                                for s, d, m in dests], local_sem=sem.rsent)
 
-    total = NB * STEPS
-    for x in range(total + 2):
-        if 0 <= x - 2 < total and x >= total:
+    before = {}
+    bring(0)
+    for x, (b, t) in enumerate(seq):
+        if b in before:
+            cast(before[b])
+            weigh(before[b])
+        before[b] = x
+        if x + 1 < len(seq) and seq[x + 1][1] == 0:
+            ahead = seq[x + 1][0]
+        else:
+            ahead = None
+        tight = t > 0 and 2 <= x < len(seq) - 1 and seq[x + 1][0] == seq[x - 2][0] and state["cast"] < x - 2
+        gather(x, 0, CUT if tight else NC)
+        if tight:
             cast(x - 2)
-        if x < total:
-            gather(x)
-            if 0 <= x - 2:
-                cast(x - 2)
-        if 0 <= x - 1 < total:
             move(x - 1)
-        if 0 <= x - 2 < total:
-            weigh(x - 2)
+            gather(x, CUT, NC)
+        turn(x)
+        if ahead is not None:
+            bring(ahead)
+        move(x - 1)
+        cast(x - 2)
+        weigh(x - 2)
+    weigh(len(seq) - 1)
 
-    for b in range(NB):
-        for bb in ([0, 1] if b < NB - 1 else [2]):
-            S.wait_ge(sem["ac%d" % bb], 2 + 2 * STEPS)
-            V.wait_ge(sem["ac%d" % bb], 2 + 2 * STEPS)
-        S.activation(T.TMP[:, 32 * b:32 * b + 32], acc(b)[:, 32:64], FN.Copy).then_inc(sem.lo, 1)
-        V.wait_ge(sem.lo, max(b + 1, 2))
-        for s in range(n_ranks):
-            V.tensor_tensor(T.OUT[:, 24 * s + 8 * b:24 * s + 8 * b + 8], acc(b)[:, s:32:4],
-                            T.TMP[:, 32 * b + s:32 * b + 32:4], OP.add).then_inc(sem.oa, 1)
-    g.wait_ge(sem.oa, NB * n_ranks)
-    g.remote_dma_fused([RemoteDMATransfer(dst_ids=[d], dma_engine_mask=m, remote_sem=sem["ra%d" % rank],
-                                          src=T.OUT[:, 24 * s:24 * s + 24], dst=T["L%d" % rank][:, :])
-                        for s, d, m in dests], local_sem=sem.rsent)
-    V.wait_ge(sem.oa, NB * n_ranks)
-    prev = T.OUT[:, 0:24]
-    for n, r in enumerate(peers):
-        V.wait_ge(sem["ra%d" % r], EPD)
-        if n:
-            V.wait_ge(sem.fin, n)
-        V.tensor_tensor(T.SUM[:, :], prev, T["L%d" % r][:, :], OP.add).then_inc(sem.fin, 1)
-        prev = T.SUM[:, :]
-    PE.wait_ge(sem.fin, 3)
-    PE.matmul(T.BK0[0:24, 0:128], T.SUM[:, :], T.IDF[:, :], True, True).then_inc(sem.fq, 1)
-    V.wait_ge(sem.fq, 1)
-    V.tensor_copy(T.YS[0:24, :], T.BK0[0:24, 0:128]).then_inc(sem.hl, 1)
-    for b, q in enumerate((Y, S, Y)):
-        q.wait_ge(sem.hl, 1)
-        q.dma_start(T.y[:, 128 * b:128 * b + 128], T.YS[8 * b:8 * b + 8, :]).then_inc(sem.yd, 16)
-    Y.wait_ge(sem.yd, 48)
+    wait(V, "ac0")
+    inc(V.tensor_copy(T.OW[0:NQ, :], acc(0)), "ow")
+    for n in range(1, NB + 1):
+        if n < NB:
+            PE.wait_ge(sem["ra%d" % src[n]], EPD)
+        else:
+            wait(PE, "ow")
+        part = T["L%d" % src[n]] if n < NB else T.OW
+        ins = PE.matmul(T.RL[0:32, 0:NQ // 8, :], part[0:NQ, :], T.IDF[0:NQ, 0:NQ], n == 1, n == NB)
+    inc(ins, "fq")
+    wait(V, "fq")
+    inc(V.tensor_copy(T.YS[0:32, :], T.RL[0:32, 0:NQ // 8, :]), "hl")
+    for e, q in enumerate((Y, S)):
+        wait(q, "hl")
+        inc(q.dma_start(T.y[e::2, :], T.YS[e:32:2, :]), "yd", 16)
+    wait(Y, "yd")
     g.wait_ge(sem.psent, 3 * EPD)
     g.wait_ge(sem.rsent, 3 * EPD)

@@ -10,8 +10,10 @@ NC = NL // 16
 STEPS = 15
 M = 4096
 WIN = 4104
-WC = 4
+FILL = (0, 1280, 2432, 3584, M)
+LOADS = ((0,), (1,), (2, 3))
 CUT = 16
+LEAD = 0
 TAIL = 1
 EPD = 4
 BIG = 8192.0
@@ -38,12 +40,12 @@ SCRATCH = {
     "B8": ("sbuf", [128, 32], "float32"),
     "IDF": ("sbuf", [128, 128], "float32"),
     "SEL": ("sbuf", [128, 96], "float16"),
+    "NSEL": ("sbuf", [128, 96], "float16"),
     "S64": ("sbuf", [128, 96], "float16"),
     "NS64": ("sbuf", [128, 96], "float16"),
     "RA": ("sbuf", [128, 40], "float16"),
     "RB": ("sbuf", [128, 40], "float16"),
     "R0": ("sbuf", [128, 64], "float16"),
-    "NSEL": ("sbuf", [128, 96], "float16"),
     "OUT": ("sbuf", [128, 96], "float32"),
     "OW": ("sbuf", [128, 32], "float32"),
     "YS": ("sbuf", [128, 96], "float32"),
@@ -63,19 +65,19 @@ for _b in range(NB):
     SCRATCH["L%d" % _b] = ("sbuf", [128, 32], "float32")
 
 SEMAPHORES = ["xld", "xwld", "nld", "wld", "xf", "v", "iot", "rs", "pc", "psent", "rsent", "oa", "ow", "fq", "hl", "yd"]
-SEMAPHORES += ["fw%d" % c for c in range(WC)]
+SEMAPHORES += ["fw%d" % c for c in range(4)]
 for _b in range(NB):
     SEMAPHORES += ["%s%d" % (n, _b) for n in ("rl", "cu", "cc", "gg", "mm", "mn", "ee", "hw", "ac", "pa", "ra")]
 
 
 def slots():
-    out = [(0, 0), (1, 0), (0, 1), (2, 0), (3, 0)]
-    own = 2
+    out = [(0, t) for t in range(LEAD + 1)] + [(b, 0) for b in range(1, NB)]
+    own = LEAD + 1
     for t in range(1, STEPS):
-        out += [(b, t) for b in range(1, NB)]
-        if own < STEPS - TAIL and t < STEPS - 1:
+        if own < STEPS - TAIL:
             out.append((0, own))
             own += 1
+        out += [(b, t) for b in range(1, NB)]
     return out + [(0, t) for t in range(own, STEPS)]
 
 
@@ -106,7 +108,6 @@ def rank_program(g, core, T, topo):
         rid, pid, _se = topo.addr(c)
         dests.append((s, DstId(rid=rid, pnc=pid), sum(1 << x for x in e)))
 
-    w = M // WC
     KF, OH = T.KF, T.OH
 
     def col(j):
@@ -118,8 +119,11 @@ def rank_program(g, core, T, topo):
     def v(ins):
         return inc(ins, "v")
 
-    def vsync():
-        wait(V, "v")
+    def scaled(out, mask, c):
+        return inc(S.activation(out, mask, FN.Copy, scale=c), "rs")
+
+    def block(R, n):
+        return R[:, n:16:2] if n < 2 else R[:, 8 * n:8 * n + 8]
 
     inc(Y.dma_start(T.XI[0:96, :], T.pts[:, :]), "xld", 16)
     inc(Y.dma_start(T.XW[:, :], T.nodes[7::16, :]), "xwld", 16)
@@ -131,27 +135,31 @@ def rank_program(g, core, T, topo):
     inc(g.iota(T.SI[:, :, 12:16], [[0, 32]], 999, 0), "iot")
     inc(g.iota(T.XN[:, :], [[1, 256]], 0, 256), "iot")
 
-    inc(V.memset(T.W[:, 0:w], 0), "fw0")
     nn = v(V.memset(T.NN[:, :], 0))
-    v(V.memset(T.XF[96:128, :], 0.0))
+    pad = v(V.memset(T.XF[96:128, :], 0.0))
+    inc(V.memset(T.W[:, 0:FILL[1]], 0), "fw0")
     wait(V, "iot", first)
     v(V.tensor_scalar(T.KI[:, 1:2], T.KI[:, 0:1], 15, None, OP.bitwise_and))
-    v(V.tensor_scalar(T.KI[:, 2:3], T.KI[:, 0:1], 4, None, OP.arith_shift_right))
-    v(V.memset(T.OUT[96:128, :], 0.0))
-    vsync()
-    v(V.tensor_copy(KF[:, 0:3], T.KI[:, 0:3]))
-    for b in range(NB):
-        v(V.memset(T["IN%d" % b][:, :, :], 0.0))
-    vsync()
-    p_, r_, g_ = col(0), col(1), col(2)
-    v(V.tensor_scalar(OH[:, :], T.CI[:, 0:16], r_, None, OP.is_equal))
-    v(V.tensor_scalar(KF[:, 4:8], T.CI[:, 3:13:3], r_, None, OP.is_gt))
-    v(V.tensor_scalar(T.B8[:, :], T.CH[:, :], g_, None, OP.is_equal))
-    v(V.tensor_scalar(T.IDF[:, :], T.CI[:, :], p_, None, OP.is_equal))
+    n = v(V.tensor_scalar(T.KI[:, 2:3], T.KI[:, 0:1], 4, None, OP.arith_shift_right))
+    v(V.memset(T.IN0[:, :, :], 0.0))
+    v(V.memset(T.RB[:, 0:16], 0.0))
+    wait(V, "v", n)
+    n = v(V.tensor_copy(KF[:, 0:3], T.KI[:, 0:3]))
+    v(V.memset(T.IN1[:, :, :], 0.0))
     wait(V, "xld")
     inc(V.tensor_copy(T.XF[0:96, :], T.XI[0:96, :]), "xf")
-    vsync()
-    masks = count["v"]
+    wait(V, "v", n)
+    p_, r_, g_ = col(0), col(1), col(2)
+    v(V.tensor_scalar(OH[:, :], T.CI[:, 0:16], r_, None, OP.is_equal))
+    n = v(V.tensor_scalar(KF[:, 4:8], T.CI[:, 3:13:3], r_, None, OP.is_gt))
+    v(V.tensor_scalar(T.B8[:, :], T.CH[:, :], g_, None, OP.is_equal))
+    masks = v(V.tensor_scalar(T.IDF[:, :], T.CI[:, :], p_, None, OP.is_equal))
+    wait(V, "xwld")
+    v(V.tensor_scalar(T.HI[:, :], T.XW[:, :], 6, None, OP.arith_shift_right))
+    v(V.tensor_scalar(T.LO[:, :], T.XW[:, :], 63, None, OP.bitwise_and))
+    wait(V, "iot")
+    rows = v(V.tensor_scalar(T.NP[:, :], T.XN[:, :], M - 1, None, OP.bitwise_and))
+    wait(V, "v", n)
     lt3, lt6, lt9, lt12 = col(4), col(5), col(6), col(7)
     v(V.tensor_scalar(col(8), lt3, 2.0, lt6, OP.mult, OP.subtract))
     v(V.tensor_scalar(col(9), lt9, 2.0, lt12, OP.mult, OP.subtract))
@@ -160,52 +168,32 @@ def rank_program(g, core, T, topo):
     v(V.tensor_scalar(col(12), oh(15), -3 * BIG, None, OP.mult))
     v(V.tensor_scalar(col(13), oh(15), -6 * BIG, None, OP.mult))
     v(V.tensor_scalar(col(14), oh(13), -1.0, None, OP.mult))
-    v(V.tensor_scalar(col(15), oh(6), oh(7), oh(8), OP.add, OP.add))
-    v(V.tensor_scalar(col(16), oh(9), -2047.0, None, OP.mult))
-    v(V.tensor_scalar(col(17), oh(6), oh(10), -2048.0, OP.add, OP.mult))
-    for n, (k, row, op) in enumerate(((13.0, 6, OP.add), (12.0, 7, OP.add), (12.0, 8, OP.add), (12.0, 7, OP.subtract))):
-        v(V.tensor_scalar(col(19 + n), oh(10), k, oh(row), OP.mult, op))
-    v(V.tensor_scalar(col(35), oh(14), -2.0, None, OP.mult))
-    v(V.memset(T.RB[:, 0:16], 0.0))
-    v(V.tensor_scalar(T.W[:, M:M + 1], lt3, 2.0 ** 22, float(M), OP.mult, OP.add))
-    vsync()
-    v(V.tensor_scalar(col(23), col(8), col(9), lt6, OP.add, OP.subtract))
-    v(V.tensor_scalar(col(24), col(8), -BIG, None, OP.mult))
-    v(V.tensor_scalar(col(18), col(19), oh(9), None, OP.subtract))
-    v(V.tensor_scalar(col(25), col(8), -BIG, col(12), OP.mult, OP.add))
-    v(V.tensor_scalar(col(26), col(15), oh(9), None, OP.add))
-    v(V.tensor_scalar(col(27), col(16), col(17), None, OP.add))
-    wait(V, "xwld")
-    v(V.tensor_scalar(T.HI[:, :], T.XW[:, :], 6, None, OP.arith_shift_right))
-    v(V.tensor_scalar(T.LO[:, :], T.XW[:, :], 63, None, OP.bitwise_and))
-    wait(V, "iot")
-    rows = v(V.tensor_scalar(T.NP[:, :], T.XN[:, :], M - 1, None, OP.bitwise_and))
+    n = v(V.tensor_scalar(col(35), oh(14), -2.0, None, OP.mult))
     for u in range(4):
         place = v(V.tensor_scalar(T.SP[:, 8 * u:8 * u + 8, :], T.SI[:, :, :], float(-u), None, OP.is_equal))
-    wait(V, "v", rows)
-    v(V.tensor_scalar(col(28), col(23), lt12, 0.5, OP.subtract, OP.mult))
-    v(V.tensor_scalar(col(29), col(23), -BIG, col(13), OP.mult, OP.add))
+    wait(V, "v", n)
+    v(V.tensor_scalar(col(23), col(8), col(9), lt6, OP.add, OP.subtract))
+    v(V.tensor_scalar(col(25), col(8), -BIG, col(12), OP.mult, OP.add))
 
     wait(g, "xf")
-    wait(g, "v", masks)
+    wait(g, "v", pad)
     g.remote_dma_fused([RemoteDMATransfer(dst_ids=[d], dma_engine_mask=m, remote_sem=sem["pa%d" % rank],
                                           src=T.XF[:, :], dst=T["XR%d" % rank][:, :]) for s, d, m in dests],
                        local_sem=sem.psent)
-    inc(g.iota(T.W[:, 3 * w:4 * w], [[0, w]], 0, 0), "fw3")
+    inc(g.iota(T.W[:, FILL[3]:M], [[0, M - FILL[3]]], 0, 0), "fw3")
 
     wait(Y, "v", nn)
     for n, shift in enumerate((0, 6, 7)):
         inc(Y.dma_start(T.NN[shift:128, 4 * n:4 * n + 2], T.nodes[0:128 - shift, 0:2]), "nld", 16)
     wait(S, "fw0")
     for c in (1, 2):
-        inc(S.activation(T.W[:, w * c:w * c + w], T.W[:, 0:w], FN.Copy), "fw%d" % c)
-    wait(Y, "fw1")
-    wait(Y, "fw2")
-    for a in range(7):
-        inc(Y.dma_start(T.W[a::16, 0:3 * w], T.nodes[a::16, 0:3 * w]), "wld", 16)
-    wait(Y, "fw3")
-    for a in range(7):
-        inc(Y.dma_start(T.W[a::16, 3 * w:M], T.nodes[a::16, 3 * w:M]), "wld", 16)
+        inc(S.activation(T.W[:, FILL[c]:FILL[c + 1]], T.W[:, 0:FILL[c + 1] - FILL[c]], FN.Copy), "fw%d" % c)
+    for parts in LOADS:
+        for c in parts:
+            wait(Y, "fw%d" % (c or 2))
+        lo, hi = FILL[parts[0]], FILL[parts[-1] + 1]
+        for a in range(7):
+            inc(Y.dma_start(T.W[a::16, lo:hi], T.nodes[a::16, lo:hi]), "wld", 16)
     wait(Y, "v", rows)
     for a, t in ((7, T.HI), (8, T.LO), (9, T.NP)):
         inc(Y.dma_start(T.W[a::16, 0:M], t[:, :]), "wld", 16)
@@ -214,42 +202,54 @@ def rank_program(g, core, T, topo):
     v(V.tensor_scalar(T.NH[:, 0:2], T.NN[:, 4:6], 6, None, OP.arith_shift_right))
     v(V.tensor_scalar(T.NH[:, 2:4], T.NN[:, 8:10], 63, None, OP.bitwise_and))
     v(V.tensor_scalar(col(30), T.NN[:, 0:1], lt6, col(11), OP.mult, OP.add))
-    v(V.tensor_scalar(col(31), T.NN[:, 5:6], 2048.0, oh(12), OP.subtract, OP.mult))
-    vsync()
+    n = v(V.tensor_scalar(col(31), T.NN[:, 5:6], 2048.0, oh(12), OP.subtract, OP.mult))
+    v(V.tensor_scalar(col(15), oh(6), oh(7), oh(8), OP.add, OP.add))
+    v(V.tensor_scalar(col(16), oh(9), -2047.0, None, OP.mult))
+    v(V.tensor_scalar(col(17), oh(6), oh(10), -2048.0, OP.add, OP.mult))
+    v(V.tensor_scalar(col(19), oh(10), 13.0, oh(6), OP.mult, OP.add))
+    wait(V, "v", n)
+    v(V.tensor_scalar(col(28), col(23), lt12, 0.5, OP.subtract, OP.mult))
     v(V.tensor_scalar(col(33), T.NN[:, 5:6], col(10), col(30), OP.mult, OP.add))
-    v(V.tensor_scalar(col(40), col(31), col(29), col(35), OP.add, OP.add))
+    n = v(V.tensor_scalar(col(29), col(23), -BIG, col(13), OP.mult, OP.add))
     v(V.tensor_scalar(col(41), col(31), col(25), None, OP.subtract))
-    for n, (node, c) in enumerate(((1, 29), (0, 25))):
-        for k, (at, row) in enumerate(((0, oh(13)), (2, oh(14)), (0, col(14)))):
-            v(V.tensor_scalar(col(42 + 3 * n + k), T.NH[:, at + node:at + node + 1], row, col(c), OP.mult, OP.add))
-    vsync()
-    cols = v(V.tensor_scalar(col(34), col(33), col(28), None, OP.subtract))
-    vsync()
-
-    def scaled(out, mask, c):
-        return inc(S.activation(out, mask, FN.Copy, scale=c), "rs")
-
+    weights = ((0, oh(13)), (2, oh(14)), (0, col(14)))
+    for k, (at, row) in enumerate(weights):
+        v(V.tensor_scalar(col(45 + k), T.NH[:, at:at + 1], row, col(25), OP.mult, OP.add))
+    wait(V, "v", n)
+    bounds = v(V.tensor_scalar(col(34), col(33), col(28), None, OP.subtract))
+    v(V.tensor_scalar(col(40), col(31), col(29), col(35), OP.add, OP.add))
+    for k, (at, row) in enumerate(weights):
+        cols = v(V.tensor_scalar(col(42 + k), T.NH[:, at + 1:at + 2], row, col(29), OP.mult, OP.add))
+    wait(V, "v", bounds)
     wait(S, "v", masks)
-    def block(R, n):
-        return R[:, n:16:2] if n < 2 else R[:, 8 * n:8 * n + 8]
-
     for out, c in ((T.SEL, 1.0), (T.NSEL, -1.0), (T.S64, 64.0), (T.NS64, -64.0)):
         scaled(out[:, :], T.IDF[:, 0:96], c)
-    wait(S, "v", rows)
-    for n, c in enumerate((col(18), oh(6), col(20), col(21), col(22))):
-        scaled(block(T.RA, n), T.B8[:, 0:8], c)
-    scaled(block(T.RB, 0), T.B8[:, 0:8], col(24))
-    scaled(T.RB[:, 16:40], T.B8[:, 0:24], col(24))
     wait(S, "v", cols)
     for n in range(8):
         scaled(block(T.R0, n), T.B8[:, 0:8], col(40 + n))
 
-    land = [T.RL, T.AC1, T.RL, T["BK%d" % (NB - 1)]]
+    def later():
+        for n, (row, op) in enumerate(((7, OP.add), (8, OP.add), (7, OP.subtract))):
+            v(V.tensor_scalar(col(20 + n), oh(10), 12.0, oh(row), OP.mult, op))
+        v(V.tensor_scalar(col(18), col(19), oh(9), None, OP.subtract))
+        v(V.tensor_scalar(col(24), col(8), -BIG, None, OP.mult))
+        v(V.tensor_scalar(col(26), col(15), oh(9), None, OP.add))
+        v(V.tensor_scalar(col(27), col(16), col(17), None, OP.add))
+        n = v(V.tensor_scalar(T.W[:, M:M + 1], lt3, 2.0 ** 22, float(M), OP.mult, OP.add))
+        wait(S, "v", n)
+        for n, c in enumerate((col(18), oh(6), col(20), col(21), col(22))):
+            scaled(block(T.RA, n), T.B8[:, 0:8], c)
+        scaled(block(T.RB, 0), T.B8[:, 0:8], col(24))
+        scaled(T.RB[:, 16:40], T.B8[:, 0:24], col(24))
+        for b in range(2, NB):
+            v(V.memset(T["IN%d" % b][:, :, :], 0.0))
+        v(V.memset(T.OUT[96:128, :], 0.0))
+
+    land = [T.RL, T["BK%d" % (NB - 1)], T.AC1, T.RL]
     seq = slots()
-    state = {"moved": -1, "cast": -1, "weighed": -1, "window": False}
+    state = {"moved": -1, "cast": -1, "weighed": -1, "window": False, "matrices": False}
     copied = {}
     last_other = max(x for x, (b, t) in enumerate(seq) if b)
-
     shared = 1 + 2 * ((max(x for x, (b, t) in enumerate(seq) if t == 0) + 1) // 2)
 
     def offsets(x):
@@ -261,7 +261,7 @@ def rank_program(g, core, T, topo):
             wait(PE, "xf")
         else:
             PE.wait_ge(sem["pa%d" % src[b]], EPD)
-        if b == 2:
+        if b == NB - 1:
             wait(PE, "pc", copied[0])
         X = T.XF if b == 0 else T["XR%d" % src[b]]
         for u in range(4):
@@ -282,6 +282,7 @@ def rank_program(g, core, T, topo):
         if c0 == 0:
             if not state["window"]:
                 state["window"] = True
+                wait(V, "v")
                 wait(V, "wld")
                 wait(S, "wld")
             if t == 1:
@@ -299,14 +300,17 @@ def rank_program(g, core, T, topo):
         bank = T["BK" + B]
         C, G = T["C" + B], T["G" + B]
         if x == 0:
-            wait(PE, "rs")
+            wait(PE, "rs", matrices)
         if t == 0:
             wait(PE, "cc" + B)
-            if land[b].name == bank.name:
-                wait(PE, "pc", copied[b])
+            if b == NB - 1:
+                wait(PE, "pc", copied[1])
             for i in range(4):
                 ins = PE.matmul(bank[0:NQ, 0:32, 2 * i:2 * i + 2], C[:, i::4], T.R0[:, :], i == 0, i == 3)
         else:
+            if not state["matrices"]:
+                state["matrices"] = True
+                wait(PE, "rs")
             wait(PE, "gg" + B)
             for i in range(4):
                 PE.matmul(bank[0:NQ, 0:20, 2 * i:2 * i + 2], G[:, i::4], T.RA[:, :], i == 0, False)
@@ -326,6 +330,8 @@ def rank_program(g, core, T, topo):
             return
         IN = T["IN" + B]
         wait(V, "mm" + B)
+        if t == 0:
+            wait(V, "v")
         inc(V.tensor_scalar(IN[0:NQ, 3:35:4, :], T["BK" + B][0:NQ, 0:8, :], -2048.0, None, OP.max), "mn" + B)
         for y in (x - 2, x - 1):
             if y >= 0 and offsets(y) == offsets(x):
@@ -370,20 +376,24 @@ def rank_program(g, core, T, topo):
             wait(S, "ac" + B)
         n = 192 if t == 0 else 96
         inc(S.activation(H[0:NQ, 0:n], T["BK" + B][0:NQ, 8:8 + n // 8, :], FN.Relu), "hw" + B)
+        if (b, t) == (1, 0):
+            wait(PE, "pc", copied[2])
         wait(PE, "hw" + B)
         for h in range(n // 32):
             ins = PE.matmul(acc(b), (T.S64, T.SEL, T.NS64)[h % 3][0:NQ, :], H[0:NQ, 32 * h:32 * h + 32],
                             t == 0 and h == 0 and b < 2, h == 2 and t == STEPS - 1 and (b == 0 or x == last_other))
         inc(ins, "ac" + B)
-        if x == last_other:
-            for bb in range(1, NB):
-                wait(S, "ac%d" % bb)
-            inc(S.activation(T.OUT[0:NQ, :], T.AC1[0:NQ, 0:12, :], FN.Copy), "oa")
-            wait(g, "oa")
-            g.remote_dma_fused([RemoteDMATransfer(dst_ids=[d], dma_engine_mask=m, remote_sem=sem["ra%d" % rank],
-                                                  src=T.OUT[:, 32 * s - 32:32 * s], dst=T["L%d" % rank][:, :])
-                                for s, d, m in dests], local_sem=sem.rsent)
 
+    def send():
+        for b in range(1, NB):
+            wait(V, "ac%d" % b)
+        inc(V.tensor_copy(T.OUT[0:NQ, :], T.AC1[0:NQ, 0:12, :]), "oa")
+        wait(g, "oa")
+        g.remote_dma_fused([RemoteDMATransfer(dst_ids=[d], dma_engine_mask=m, remote_sem=sem["ra%d" % rank],
+                                              src=T.OUT[:, 32 * s - 32:32 * s], dst=T["L%d" % rank][:, :])
+                            for s, d, m in dests], local_sem=sem.rsent)
+
+    matrices = count["rs"]
     before = {}
     bring(0)
     for x, (b, t) in enumerate(seq):
@@ -391,22 +401,26 @@ def rank_program(g, core, T, topo):
             cast(before[b])
             weigh(before[b])
         before[b] = x
-        if x + 1 < len(seq) and seq[x + 1][1] == 0:
-            ahead = seq[x + 1][0]
-        else:
-            ahead = None
+        if (b, t) == (1, 0):
+            cast(x - 1)
+            bring(1)
+            bring(2)
         tight = t > 0 and 2 <= x < len(seq) - 1 and seq[x + 1][0] == seq[x - 2][0] and state["cast"] < x - 2
         gather(x, 0, CUT if tight else NC)
+        if x == 0:
+            later()
+        if x == last_other + 1:
+            send()
         if tight:
             cast(x - 2)
             move(x - 1)
             gather(x, CUT, NC)
         turn(x)
-        if ahead is not None:
-            bring(ahead)
+        if (b, t) == (1, 0):
+            bring(3)
         move(x - 1)
         cast(x - 2)
-        weigh(x - 2)
+        weigh(x if x == last_other else x - 2)
     weigh(len(seq) - 1)
 
     wait(V, "ac0")

@@ -8,44 +8,49 @@ NL = 384
 NQ = NL // 4
 NC = NL // 16
 STEPS = 15
+SUMMED = 13
+LEFT = 2 * (STEPS - SUMMED)
 M = 4096
 WIN = 4104
-FILL = (0, 1280, 2432, 3584, M)
-LOADS = ((0,), (1,), (2, 3))
-CUT = 16
-LEAD = 0
-TAIL = 1
+WHOLE = 768
+EARLY = 896
+FILLS = ((896, 1920), (1920, 2944), (2944, 3968), (3968, M))
+ROW_ONE, ROW_LO = 9, 12
 EPD = 4
+ALONE = 16
 BIG = 8192.0
+SHIFT = -1536
+COPIED = (3,)
+CUT = 12
 
 SCRATCH = {
     "W": ("sbuf", [128, WIN], "int32"),
-    "XI": ("sbuf", [128, 96], "int32"),
-    "XF": ("sbuf", [128, 96], "float32"),
+    "XI": ("sbuf", [128, 192], "int32"),
+    "XS": ("sbuf", [128, 192], "int32"),
+    "XF": ("sbuf", [128, 192], "float16"),
     "XW": ("sbuf", [128, 256], "int32"),
-    "HI": ("sbuf", [128, 256], "int32"),
     "LO": ("sbuf", [128, 256], "int32"),
-    "XN": ("sbuf", [128, 256], "int32"),
-    "NP": ("sbuf", [128, 256], "int32"),
-    "NN": ("sbuf", [128, 12], "int32"),
+    "NN": ("sbuf", [128, 2], "int32"),
     "NH": ("sbuf", [128, 4], "int32"),
     "P": ("sbuf", [128, NB * NL], "float32"),
     "KI": ("sbuf", [128, 4], "int32"),
-    "CI": ("sbuf", [128, 128], "int32"),
-    "CH": ("sbuf", [128, 32], "int32"),
+    "CI": ("sbuf", [128, 16], "int32"),
+    "CH": ("sbuf", [128, 16], "int32"),
     "SI": ("sbuf", [128, 8, 16], "int32"),
-    "SP": ("sbuf", [128, 32, 16], "float32"),
+    "SP": ("sbuf", [128, 16, 16], "float16"),
     "KF": ("sbuf", [128, 64], "float32"),
     "OH": ("sbuf", [128, 16], "float32"),
-    "B8": ("sbuf", [128, 32], "float32"),
-    "IDF": ("sbuf", [128, 128], "float32"),
-    "SEL": ("sbuf", [128, 96], "float16"),
-    "NSEL": ("sbuf", [128, 96], "float16"),
-    "S64": ("sbuf", [128, 96], "float16"),
-    "NS64": ("sbuf", [128, 96], "float16"),
-    "RA": ("sbuf", [128, 40], "float16"),
-    "RB": ("sbuf", [128, 40], "float16"),
-    "R0": ("sbuf", [128, 64], "float16"),
+    "B8": ("sbuf", [128, 16], "float32"),
+    "IDF": ("sbuf", [128, 96], "float32"),
+    "ID": ("sbuf", [128, 128], "float16"),
+    "ZT": ("sbuf", [128, 128], "float16"),
+    "UP": ("sbuf", [128, 96], "float16"),
+    "DOWN": ("sbuf", [128, 96], "float16"),
+    "RA": ("sbuf", [128, 32], "float16"),
+    "RB": ("sbuf", [128, 32], "float16"),
+    "RS": ("sbuf", [128, 48], "float16"),
+    "RD": ("sbuf", [128, 48], "float16"),
+    "IN": ("sbuf", [128, 32 * NB + 4, 8], "float16"),
     "OUT": ("sbuf", [128, 96], "float32"),
     "OW": ("sbuf", [128, 32], "float32"),
     "YS": ("sbuf", [128, 96], "float32"),
@@ -58,27 +63,16 @@ for _b in range(NB):
     SCRATCH["C%d" % _b] = ("sbuf", [128, NL], "float16")
     SCRATCH["G%d" % _b] = ("sbuf", [128, NL], "float16")
     SCRATCH["CU%d" % _b] = ("sbuf", [128, NC], "uint16")
-    SCRATCH["IN%d" % _b] = ("sbuf", [128, 36, 8], "float16")
-    SCRATCH["HW%d" % _b] = ("sbuf", [128, 192], "float16")
+    SCRATCH["HW%d" % _b] = ("sbuf", [128, 128], "float16")
     SCRATCH["BK%d" % _b] = ("psum", [128, 64, 8], "float32")
-    SCRATCH["XR%d" % _b] = ("sbuf", [128, 96], "float32")
+    SCRATCH["XR%d" % _b] = ("sbuf", [128, 192], "float16")
     SCRATCH["L%d" % _b] = ("sbuf", [128, 32], "float32")
+    SCRATCH["HS%d" % _b] = ("sbuf", [128, 32 * LEFT], "float16")
+    SCRATCH["HL%d" % _b] = ("sbuf", [128, 32 * LEFT], "float16")
 
-SEMAPHORES = ["xld", "xwld", "nld", "wld", "xf", "v", "iot", "rs", "pc", "psent", "rsent", "oa", "ow", "fq", "hl", "yd"]
-SEMAPHORES += ["fw%d" % c for c in range(4)]
+SEMAPHORES = ["xld", "xwld", "nld", "w0", "wld", "V", "S", "PE", "g", "sent", "yd"]
 for _b in range(NB):
-    SEMAPHORES += ["%s%d" % (n, _b) for n in ("rl", "cu", "cc", "gg", "mm", "mn", "ee", "hw", "ac", "pa", "ra")]
-
-
-def slots():
-    out = [(0, t) for t in range(LEAD + 1)] + [(b, 0) for b in range(1, NB)]
-    own = LEAD + 1
-    for t in range(1, STEPS):
-        if own < STEPS - TAIL:
-            out.append((0, own))
-            own += 1
-        out += [(b, t) for b in range(1, NB)]
-    return out + [(0, t) for t in range(own, STEPS)]
+    SEMAPHORES += ["%s%d" % (n, _b) for n in ("pa", "ra", "rb")]
 
 
 def rank_program(g, core, T, topo):
@@ -87,8 +81,8 @@ def rank_program(g, core, T, topo):
         return
     sem = T.sem
     V, S, PE, Y = g.vector, g.scalar, g.tensor, g.sync
-    n_ranks = len(T.cores)
-    src = [(rank + s) % n_ranks for s in range(n_ranks)]
+    queue = {"V": V, "S": S, "PE": PE, "g": g}
+    src = [(rank + s) % NB for s in range(NB)]
     count = {}
 
     def inc(ins, name, n=1):
@@ -99,16 +93,15 @@ def rank_program(g, core, T, topo):
     def wait(q, name, n=None):
         q.wait_ge(sem[name], count[name] if n is None else n)
 
-    order = sorted(range(1, n_ranks), key=lambda s: topo.die(T.cores[src[s]]) == topo.die(core))
-    dests = []
-    for n, s in enumerate(order):
-        c = T.cores[src[s]]
-        e = topo.engines(core, c)
-        e = (e[0::2] + e[1::2])[EPD * n:EPD * n + EPD]
-        rid, pid, _se = topo.addr(c)
-        dests.append((s, DstId(rid=rid, pnc=pid), sum(1 << x for x in e)))
+    def to(sources, a, n, name, out, in_):
+        cores = [T.cores[src[s]] for s in sources]
+        e = [x for x in topo.engines(core, cores[0]) if all(x in topo.engines(core, c) for c in cores)]
+        return RemoteDMATransfer(dst_ids=[DstId(rid=topo.addr(c)[0], pnc=topo.addr(c)[1]) for c in cores],
+                                 dma_engine_mask=sum(1 << x for x in (e[0::2] + e[1::2])[a:a + n]),
+                                 remote_sem=sem["%s%d" % (name, rank)], srcs=[in_], dsts=[out] * len(cores))
 
-    KF, OH = T.KF, T.OH
+    order = sorted(range(1, NB), key=lambda s: topo.die(T.cores[src[s]]) == topo.die(core))
+    KF, OH, ID, zeros = T.KF, T.OH, T.ID, T.ZT
 
     def col(j):
         return KF[:, j:j + 1]
@@ -117,327 +110,315 @@ def rank_program(g, core, T, topo):
         return OH[:, r:r + 1]
 
     def v(ins):
-        return inc(ins, "v")
+        return inc(ins, "V")
 
     def scaled(out, mask, c):
-        return inc(S.activation(out, mask, FN.Copy, scale=c), "rs")
+        return inc(S.activation(out, mask, FN.Copy, scale=c), "S")
 
     def block(R, n):
         return R[:, n:16:2] if n < 2 else R[:, 8 * n:8 * n + 8]
 
-    inc(Y.dma_start(T.XI[0:96, :], T.pts[:, :]), "xld", 16)
+    def mark(out, in_, step, base, value):
+        return inc(g.affine_select(out, in_, [[-step, out.shape[-1]]], OP.not_equal, value, -base, 1), "g")
+
+    inc(Y.dma_start(T.XI[0:48, :], T.pts[:, :]), "xld", 16)
+    inc(S.dma_start(T.XI[64:112, :], T.pts[:, :]), "xld", 16)
     inc(Y.dma_start(T.XW[:, :], T.nodes[7::16, :]), "xwld", 16)
 
-    inc(g.iota(T.KI[:, 0:1], [[1, 1]], 0, 1), "iot")
-    inc(g.iota(T.CI[:, :], [[1, 128]], 0, 0), "iot")
-    first = inc(g.iota(T.CH[:, :], [[0, 4], [1, 8]], 0, 0), "iot")
-    inc(g.iota(T.SI[:, :, 0:12], [[12, 8], [0, 4], [4, 3]], 0, -1), "iot")
-    inc(g.iota(T.SI[:, :, 12:16], [[0, 32]], 999, 0), "iot")
-    inc(g.iota(T.XN[:, :], [[1, 256]], 0, 256), "iot")
+    zero = v(V.memset(T.IN[:, :, :], 0.0))
+    pad = v(V.memset(T.XF[:, :], 0.0))
+    blank = v(V.memset(zeros[:, :], 0.0))
 
-    nn = v(V.memset(T.NN[:, :], 0))
-    pad = v(V.memset(T.XF[96:128, :], 0.0))
-    inc(V.memset(T.W[:, 0:FILL[1]], 0), "fw0")
-    wait(V, "iot", first)
-    v(V.tensor_scalar(T.KI[:, 1:2], T.KI[:, 0:1], 15, None, OP.bitwise_and))
-    n = v(V.tensor_scalar(T.KI[:, 2:3], T.KI[:, 0:1], 4, None, OP.arith_shift_right))
-    v(V.memset(T.IN0[:, :, :], 0.0))
-    v(V.memset(T.RB[:, 0:16], 0.0))
-    wait(V, "v", n)
-    n = v(V.tensor_copy(KF[:, 0:3], T.KI[:, 0:3]))
-    v(V.memset(T.IN1[:, :, :], 0.0))
+    inc(g.iota(T.KI[:, 0:1], [[1, 1]], 0, 1), "g")
+    first = inc(g.iota(T.CI[:, :], [[1, 16]], 0, 0), "g")
+    inc(g.iota(T.CH[:, :], [[0, 2], [1, 8]], 0, 0), "g")
+    inc(g.iota(T.SI[:, :, 0:12], [[6, 8], [0, 4], [2, 3]], 0, 0), "g")
+    patterns = inc(g.iota(T.SI[:, :, 12:16], [[0, 32]], 999, 0), "g")
+    wait(g, "V", blank)
+    ident = mark(ID[:, :], zeros[:, :], 1, 0, 1.0)
+    cleared = mark(T.RB[:, 0:16], zeros[:, 0:16], 0, -1, 0.0)
+    if EARLY > WHOLE:
+        inc(g.iota(T.W[:, WHOLE:EARLY], [[0, EARLY - WHOLE]], 0, 0), "g")
+
+    inc(Y.dma_start(T.NN[6:128, :], T.nodes[0:122, 0:2]), "nld", 16)
+    inc(Y.dma_start(T.NN[0:6, :], T.nodes[0:6, 0:2]), "nld", 16)
+    inc(Y.dma_start(T.W[:, 0:WHOLE], T.nodes[:, 0:WHOLE]), "w0", 16)
+    wait(S, "V", zero)
+    filled = [inc(S.activation(T.W[:, lo:hi], T.IN[:, 0:(hi - lo) // 8, :], FN.Copy), "S") for lo, hi in FILLS]
+    wait(Y, "g")
+    for c, lo, hi in ((0, WHOLE, FILLS[0][1]), (-1, FILLS[0][1], M)):
+        wait(Y, "S", filled[c])
+        for a in range(8):
+            inc(Y.dma_start(T.W[a::16, lo:hi], T.nodes[a::16, lo:hi]), "wld", 16)
+
+    wait(V, "g", first)
+    for j, (c, op) in enumerate(((15, OP.bitwise_and), (4, OP.arith_shift_right), (63, OP.bitwise_and))):
+        n = v(V.tensor_scalar(T.KI[:, 1 + j:2 + j], T.KI[:, 0:1], c, None, op))
     wait(V, "xld")
-    inc(V.tensor_copy(T.XF[0:96, :], T.XI[0:96, :]), "xf")
-    wait(V, "v", n)
-    p_, r_, g_ = col(0), col(1), col(2)
-    v(V.tensor_scalar(OH[:, :], T.CI[:, 0:16], r_, None, OP.is_equal))
+    split = v(V.tensor_scalar(T.XS[64:112, :], T.XI[64:112, :], 2047, None, OP.bitwise_and))
+    wait(V, "V", pad)
+    v(V.tensor_scalar(T.XF[0:48, :], T.XI[0:48, :], 2.0 ** -11, SHIFT - 0.5 + 2.0 ** -12, OP.mult, OP.add))
+    wait(V, "V", n)
+    n = v(V.tensor_copy(KF[:, 1:4], T.KI[:, 1:4]))
+    wait(V, "V", split)
+    points = v(V.tensor_scalar(T.XF[64:112, :], T.XS[64:112, :], 2.0 ** -11, None, OP.mult))
+    wait(V, "V", n)
+    r_, g_ = col(1), col(2)
+    v(V.tensor_scalar(OH[:, :], T.CI[:, :], r_, None, OP.is_equal))
     n = v(V.tensor_scalar(KF[:, 4:8], T.CI[:, 3:13:3], r_, None, OP.is_gt))
+    wait(V, "g", patterns)
     v(V.tensor_scalar(T.B8[:, :], T.CH[:, :], g_, None, OP.is_equal))
-    masks = v(V.tensor_scalar(T.IDF[:, :], T.CI[:, :], p_, None, OP.is_equal))
-    wait(V, "xwld")
-    v(V.tensor_scalar(T.HI[:, :], T.XW[:, :], 6, None, OP.arith_shift_right))
-    v(V.tensor_scalar(T.LO[:, :], T.XW[:, :], 63, None, OP.bitwise_and))
-    wait(V, "iot")
-    rows = v(V.tensor_scalar(T.NP[:, :], T.XN[:, :], M - 1, None, OP.bitwise_and))
-    wait(V, "v", n)
+    for h in range(2):
+        place = v(V.tensor_scalar(T.SP[:, 8 * h:8 * h + 8, :], T.SI[:, :, :], float(h), col(3), OP.add, OP.is_equal))
+    wait(V, "V", n)
     lt3, lt6, lt9, lt12 = col(4), col(5), col(6), col(7)
     v(V.tensor_scalar(col(8), lt3, 2.0, lt6, OP.mult, OP.subtract))
-    v(V.tensor_scalar(col(9), lt9, 2.0, lt12, OP.mult, OP.subtract))
+    v(V.tensor_scalar(col(9), lt3, lt6, lt9, OP.subtract, OP.add))
     v(V.tensor_scalar(col(10), lt12, lt6, None, OP.subtract))
-    v(V.tensor_scalar(col(11), lt12, -1.0, 1.0, OP.mult, OP.add))
-    v(V.tensor_scalar(col(12), oh(15), -3 * BIG, None, OP.mult))
-    v(V.tensor_scalar(col(13), oh(15), -6 * BIG, None, OP.mult))
-    v(V.tensor_scalar(col(14), oh(13), -1.0, None, OP.mult))
-    n = v(V.tensor_scalar(col(35), oh(14), -2.0, None, OP.mult))
-    for u in range(4):
-        place = v(V.tensor_scalar(T.SP[:, 8 * u:8 * u + 8, :], T.SI[:, :, :], float(-u), None, OP.is_equal))
-    wait(V, "v", n)
-    v(V.tensor_scalar(col(23), col(8), col(9), lt6, OP.add, OP.subtract))
-    v(V.tensor_scalar(col(25), col(8), -BIG, col(12), OP.mult, OP.add))
-
-    wait(g, "xf")
-    wait(g, "v", pad)
-    g.remote_dma_fused([RemoteDMATransfer(dst_ids=[d], dma_engine_mask=m, remote_sem=sem["pa%d" % rank],
-                                          src=T.XF[:, :], dst=T["XR%d" % rank][:, :]) for s, d, m in dests],
-                       local_sem=sem.psent)
-    inc(g.iota(T.W[:, FILL[3]:M], [[0, M - FILL[3]]], 0, 0), "fw3")
-
-    wait(Y, "v", nn)
-    for n, shift in enumerate((0, 6, 7)):
-        inc(Y.dma_start(T.NN[shift:128, 4 * n:4 * n + 2], T.nodes[0:128 - shift, 0:2]), "nld", 16)
-    wait(S, "fw0")
-    for c in (1, 2):
-        inc(S.activation(T.W[:, FILL[c]:FILL[c + 1]], T.W[:, 0:FILL[c + 1] - FILL[c]], FN.Copy), "fw%d" % c)
-    for parts in LOADS:
-        for c in parts:
-            wait(Y, "fw%d" % (c or 2))
-        lo, hi = FILL[parts[0]], FILL[parts[-1] + 1]
-        for a in range(7):
-            inc(Y.dma_start(T.W[a::16, lo:hi], T.nodes[a::16, lo:hi]), "wld", 16)
-    wait(Y, "v", rows)
-    for a, t in ((7, T.HI), (8, T.LO), (9, T.NP)):
-        inc(Y.dma_start(T.W[a::16, 0:M], t[:, :]), "wld", 16)
-
+    n = v(V.tensor_scalar(KF[:, 12:14], T.CI[:, 3:7:3], oh(15), -BIG, OP.mult, OP.mult))
+    wait(V, "xwld")
+    v(V.tensor_scalar(T.LO[:, :], T.XW[:, :], 127, None, OP.bitwise_and))
+    wait(V, "V", n)
+    v(V.tensor_scalar(col(23), col(9), 2.0, lt12, OP.mult, OP.subtract))
+    v(V.tensor_scalar(col(30), lt12, -2048.0 * SHIFT, -0.5, OP.mult, OP.add))
+    n = v(V.tensor_scalar(col(25), col(8), -BIG, col(12), OP.mult, OP.add))
     wait(V, "nld")
-    v(V.tensor_scalar(T.NH[:, 0:2], T.NN[:, 4:6], 6, None, OP.arith_shift_right))
-    v(V.tensor_scalar(T.NH[:, 2:4], T.NN[:, 8:10], 63, None, OP.bitwise_and))
-    v(V.tensor_scalar(col(30), T.NN[:, 0:1], lt6, col(11), OP.mult, OP.add))
-    n = v(V.tensor_scalar(col(31), T.NN[:, 5:6], 2048.0, oh(12), OP.subtract, OP.mult))
-    v(V.tensor_scalar(col(15), oh(6), oh(7), oh(8), OP.add, OP.add))
-    v(V.tensor_scalar(col(16), oh(9), -2047.0, None, OP.mult))
-    v(V.tensor_scalar(col(17), oh(6), oh(10), -2048.0, OP.add, OP.mult))
-    v(V.tensor_scalar(col(19), oh(10), 13.0, oh(6), OP.mult, OP.add))
-    wait(V, "v", n)
-    v(V.tensor_scalar(col(28), col(23), lt12, 0.5, OP.subtract, OP.mult))
-    v(V.tensor_scalar(col(33), T.NN[:, 5:6], col(10), col(30), OP.mult, OP.add))
-    n = v(V.tensor_scalar(col(29), col(23), -BIG, col(13), OP.mult, OP.add))
-    v(V.tensor_scalar(col(41), col(31), col(25), None, OP.subtract))
-    weights = ((0, oh(13)), (2, oh(14)), (0, col(14)))
-    for k, (at, row) in enumerate(weights):
-        v(V.tensor_scalar(col(45 + k), T.NH[:, at:at + 1], row, col(25), OP.mult, OP.add))
-    wait(V, "v", n)
-    bounds = v(V.tensor_scalar(col(34), col(33), col(28), None, OP.subtract))
-    v(V.tensor_scalar(col(40), col(31), col(29), col(35), OP.add, OP.add))
-    for k, (at, row) in enumerate(weights):
-        cols = v(V.tensor_scalar(col(42 + k), T.NH[:, at + 1:at + 2], row, col(29), OP.mult, OP.add))
-    wait(V, "v", bounds)
-    wait(S, "v", masks)
-    for out, c in ((T.SEL, 1.0), (T.NSEL, -1.0), (T.S64, 64.0), (T.NS64, -64.0)):
-        scaled(out[:, :], T.IDF[:, 0:96], c)
-    wait(S, "v", cols)
-    for n in range(8):
-        scaled(block(T.R0, n), T.B8[:, 0:8], col(40 + n))
+    v(V.tensor_scalar(T.NH[:, 0:2], T.NN[:, :], 7, None, OP.arith_shift_right))
+    halves = v(V.tensor_scalar(T.NH[:, 2:4], T.NN[:, :], 127, None, OP.bitwise_and))
+    wait(V, "V", n)
+    n = v(V.tensor_scalar(col(28), col(23), 0.5, col(30), OP.mult, OP.add))
+    fixed = v(V.tensor_scalar(col(29), col(23), -BIG, col(13), OP.mult, OP.add))
+    v(V.tensor_scalar(col(40), T.NN[:, 1:2], -2050.0, None, OP.add))
+    wait(V, "V", halves)
+    v(V.tensor_scalar(KF[:, 42:44], T.NH[:, 2:4], 512.0, None, OP.add))
+    high = v(V.tensor_scalar(KF[:, 46:48], T.NH[:, 0:2], -1.0, 4.0, OP.mult, OP.add))
+    wait(V, "V", n)
+    wait(V, "w0")
+    read = v(V.tensor_scalar(col(33), T.W[:, 0:1], lt6, col(28), OP.mult, OP.subtract))
+    v(V.tensor_scalar(col(41), T.NN[:, 1:2], -1.0, 2048.0, OP.mult, OP.add))
+    v(V.tensor_scalar(col(26), lt6, -1 / 128, 1 / 128, OP.mult, OP.add))
+    wait(V, "V", high)
+    cols = v(V.tensor_tensor(KF[:, 44:46], KF[:, 42:44], KF[:, 46:48], OP.add))
+    v(V.tensor_scalar(col(27), oh(7), 16 + SHIFT - 0.5 + 2.0 ** -8, -16.0, OP.mult, OP.add))
+    wait(V, "V", read)
+    bounds = v(V.tensor_scalar(col(34), T.NN[:, 1:2], col(10), col(33), OP.mult, OP.add))
 
     def later():
-        for n, (row, op) in enumerate(((7, OP.add), (8, OP.add), (7, OP.subtract))):
-            v(V.tensor_scalar(col(20 + n), oh(10), 12.0, oh(row), OP.mult, op))
-        v(V.tensor_scalar(col(18), col(19), oh(9), None, OP.subtract))
-        v(V.tensor_scalar(col(24), col(8), -BIG, None, OP.mult))
-        v(V.tensor_scalar(col(26), col(15), oh(9), None, OP.add))
-        v(V.tensor_scalar(col(27), col(16), col(17), None, OP.add))
-        n = v(V.tensor_scalar(T.W[:, M:M + 1], lt3, 2.0 ** 22, float(M), OP.mult, OP.add))
-        wait(S, "v", n)
-        for n, c in enumerate((col(18), oh(6), col(20), col(21), col(22))):
-            scaled(block(T.RA, n), T.B8[:, 0:8], c)
-        scaled(block(T.RB, 0), T.B8[:, 0:8], col(24))
-        scaled(T.RB[:, 16:40], T.B8[:, 0:24], col(24))
-        for b in range(2, NB):
-            v(V.memset(T["IN%d" % b][:, :, :], 0.0))
-        v(V.memset(T.OUT[96:128, :], 0.0))
+        V.tensor_scalar(col(32), col(34), col(28), None, OP.add)
+        return V.tensor_scalar(T.W[:, M:M + 1], col(8), 2.0 ** 22, float(M), OP.mult, OP.add)
 
-    land = [T.RL, T["BK%d" % (NB - 1)], T.AC1, T.RL]
-    seq = slots()
-    state = {"moved": -1, "cast": -1, "weighed": -1, "window": False, "matrices": False}
-    copied = {}
-    last_other = max(x for x, (b, t) in enumerate(seq) if b)
-    shared = 1 + 2 * ((max(x for x, (b, t) in enumerate(seq) if t == 0) + 1) // 2)
+    wait(g, "V", points)
+    g.remote_dma_fused([to(range(NB - 1, 0, -1), 0, ALONE, "pa", T["XR%d" % rank][:, :], T.XF[:, :])], local_sem=sem.sent)
+    for out, c in ((T.UP, 129.0), (T.DOWN, -128.0)):
+        scales = mark(out[:, :], zeros[:, 0:NQ], 1, 0, c)
+    terms = (((6, 128.0), (ROW_ONE, 1 / 16)), ((6, -128.0),), ((ROW_LO, 128.0), (ROW_ONE, -(2048 + 512) / 16)),
+             ((ROW_LO, 128.0), (7, -1.0), (ROW_ONE, -(2048 + 516 + SHIFT) / 16)))
+    for k in range(3):
+        if k:
+            wait(g, "g")
+        for n, rows_ in enumerate(terms):
+            if k < len(rows_):
+                marked = mark(block(T.RA, n), block(T.RA, n) if k else zeros[:, 0:8], 16, *rows_[k])
+    for out in (T.IDF, T.OUT):
+        inc(g.iota(out[:, :], [[0, 96]], 0, 0, allow_small_or_imprecise_dtypes=True), "g")
+    for b in range(1, NB):
+        mark(T["HS%d" % b][:, :], zeros[:, 0:32 * LEFT], 0, -1, 0.0)
+    wait(g, "g")
+    made = mark(T.IDF[:, :], T.IDF[:, :], 1, 0, 1.0)
 
-    def offsets(x):
-        return "RL" if x >= shared and x % 2 else "CP"
+    wait(Y, "V", read)
+    inc(Y.dma_start(T.W[ROW_LO::16, 0:M], T.LO[:, :]), "wld", 16)
 
-    def bring(b):
-        if b == 0:
-            wait(PE, "v", place)
-            wait(PE, "xf")
+    wait(S, "V", fixed)
+    scaled(block(T.RS, 0), T.B8[:, 0:8], col(29))
+    scaled(block(T.RS, 1), T.B8[:, 0:8], col(25))
+    scaled(T.RS[:, 16:32], T.B8[:, :], col(29))
+    scaled(T.RS[:, 32:48], T.B8[:, :], col(25))
+    wait(S, "V", cols)
+    wait(S, "g", ident)
+    for n, (row, c) in enumerate(((12, 40), (12, 41), (13, 43), (13, 45), (13, 42), (13, 44))):
+        matrices = scaled(block(T.RD, n), ID[:, row::16], col(c))
+
+    def more():
+        S.activation(block(T.RB, 0), T.B8[:, 0:8], FN.Copy, scale=col(25))
+        return S.activation(T.RB[:, 16:32], T.B8[:, :], FN.Copy, scale=col(25))
+
+    tasks, group = {}, {}
+
+    def task(name, q, needs, call, waits=()):
+        tasks[name] = (q, needs, call, waits)
+
+    def ends(name, n):
+        group[name] = group.get(name, 0) + 1
+        return group[name] == 1, group[name] == n
+
+    def products(out, lhs, rhs, n, start, stop):
+        for i in range(n):
+            ins = PE.matmul(out(i), lhs(i), rhs(i), start and i == 0, stop and i == n - 1)
+        return ins
+
+    land = [T.CP, T.RL, T.AC1, T.CP]
+    window = T.W[:, 0:M + 1]
+    total = T.RL[0:32, 0:NQ // 8, :]
+    weights = (T.UP, T.DOWN)
+    parts = 2 * NB - 1 + STEPS - SUMMED
+
+    def source(b):
+        X, C, P = T.XF if b == 0 else T["XR%d" % src[b]], T["C%d" % b], T.P[:, NL * b:NL * b + NL]
+        task(("bring", b), "PE", [("keep", 0)] if b == NB - 1 else [], lambda: products(
+            lambda u: land[b][:, 0:NL // 8, u::4], lambda u: T.SP[:, 8 * (u // 2):8 * (u // 2) + 8, :],
+            lambda u: X[:, NQ * (u % 2):NQ * (u % 2) + NQ], 4, True, True), [("pa%d" % src[b], ALONE)] if b else [("V", place)])
+        copied = b in COPIED
+        task(("keep", b), "S", [("bring" if copied else "test", b)], lambda: S.activation(
+            P, land[b][:, 0:NL // 8, :], FN.Identity, bias=col(28), scale=2048.0))
+        if copied:
+            task(("test", b), "V", [("keep", b), "later"], lambda: V.tensor_scalar(C[:, :], P, col(32), None, OP.is_lt))
         else:
-            PE.wait_ge(sem["pa%d" % src[b]], EPD)
-        if b == NB - 1:
-            wait(PE, "pc", copied[0])
-        X = T.XF if b == 0 else T["XR%d" % src[b]]
-        for u in range(4):
-            ins = PE.matmul(land[b][:, 0:NL // 8, u::4], T.SP[0:96, 8 * u:8 * u + 8, :], X[0:96, :], u == 0, u == 3)
-        inc(ins, "rl%d" % b)
+            task(("test", b), "V", [("bring", b)], lambda: V.tensor_scalar(
+                C[:, :], land[b][:, 0:NL // 8, :], 2048.0, col(34), OP.mult, OP.is_lt), [("V", bounds)])
 
-    def gather(x, c0, c1):
-        b, t = seq[x]
-        B = str(b)
-        C = T["C" + B]
-        if t == 0:
-            wait(V, "rl" + B)
-            points = land[b][:, 0:NL // 8, :]
-            inc(V.tensor_scalar(C[:, :], points, col(34), None, OP.is_lt), "cc" + B)
-            wait(S, "cc" + B)
-            copied[b] = inc(S.activation(T.P[:, NL * b:NL * b + NL], points, FN.Identity, bias=col(28)), "pc")
-            return
-        if c0 == 0:
-            if not state["window"]:
-                state["window"] = True
-                wait(V, "v")
-                wait(V, "wld")
-                wait(S, "wld")
-            if t == 1:
-                wait(V, "pc", copied[b])
-            wait(V, "cu" + B)
-            wait(S, "cu" + B)
-            inc(S.activation(T["G" + B][:, :], T.W[:, 0:M + 1].indirect(T["CU" + B][:, :]), FN.Identity,
-                             bias=col(27), scale=col(26)), "gg" + B)
-        inc(V.tensor_tensor(C[:, 16 * c0:16 * c1], T.W[:, 0:M + 1].indirect(T["CU" + B][:, c0:c1]),
-                            T.P[:, NL * b + 16 * c0:NL * b + 16 * c1], OP.is_gt), "cc" + B)
+    def step(b, t):
+        at = 32 * b + 3
+        C, G, CU, BK, IN = T["C%d" % b], T["G%d" % b], T["CU%d" % b], T["BK%d" % b], T.IN
+        acc = T.AC1[0:NQ, 4 * b - 4:4 * b, :] if b else T.AC0[0:NQ, 0:4, :]
+        wide = 16 if t else 24
+        offsets = BK[:, 32:32 + NC // 8, :]
 
-    def turn(x):
-        b, t = seq[x]
-        B = str(b)
-        bank = T["BK" + B]
-        C, G = T["C" + B], T["G" + B]
-        if x == 0:
-            wait(PE, "rs", matrices)
+        def turn(X, R):
+            return products(lambda i: BK[0:NQ, 0:wide, 2 * i:2 * i + 2], lambda i: X[:, i::4], lambda i: R[:, :], 4,
+                            *ends(("turn", b, t), 3 if t else 2))
+
         if t == 0:
-            wait(PE, "cc" + B)
-            if b == NB - 1:
-                wait(PE, "pc", copied[1])
-            for i in range(4):
-                ins = PE.matmul(bank[0:NQ, 0:32, 2 * i:2 * i + 2], C[:, i::4], T.R0[:, :], i == 0, i == 3)
+            for name, R in (("turn G", T.RD), ("turn C", T.RS)):
+                task((name, b, 0), "PE", [("test", b)], lambda R=R: turn(C, R), [("S", matrices)])
         else:
-            if not state["matrices"]:
-                state["matrices"] = True
-                wait(PE, "rs")
-            wait(PE, "gg" + B)
-            for i in range(4):
-                PE.matmul(bank[0:NQ, 0:20, 2 * i:2 * i + 2], G[:, i::4], T.RA[:, :], i == 0, False)
-            wait(PE, "cc" + B)
-            for i in range(4):
-                ins = PE.matmul(bank[0:NQ, 0:20, 2 * i:2 * i + 2], C[:, i::4], T.RB[:, :], False, i == 3)
-        inc(ins, "mm" + B)
-
-    def move(x):
-        if x <= state["moved"]:
-            return
-        cast(x - 2)
-        state["moved"] = x
-        b, t = seq[x]
-        B = str(b)
-        if t == STEPS - 1:
-            return
-        IN = T["IN" + B]
-        wait(V, "mm" + B)
-        if t == 0:
-            wait(V, "v")
-        inc(V.tensor_scalar(IN[0:NQ, 3:35:4, :], T["BK" + B][0:NQ, 0:8, :], -2048.0, None, OP.max), "mn" + B)
-        for y in (x - 2, x - 1):
-            if y >= 0 and offsets(y) == offsets(x):
-                cast(y)
-                if seq[y][1] < STEPS - 1:
-                    wait(PE, "cu%d" % seq[y][0])
-        if x == shared:
-            wait(PE, "pc")
-        wait(PE, "mn" + B)
-        for n in range(8):
-            h, k = divmod(n, 4)
-            ins = PE.matmul(T[offsets(x)][:, 0:NC // 8, :], IN[0:NQ, 3 - k:35 - k, 1 - h::2],
-                            (T.SEL, T.NSEL)[h][0:NQ, k::4], n == 0, n == 7)
-        inc(ins, "ee" + B)
-
-    def cast(x):
-        if x <= state["cast"]:
-            return
-        move(x)
-        state["cast"] = x
-        b, t = seq[x]
-        B = str(b)
-        if t == STEPS - 1:
-            return
-        wait(V, "ee" + B)
-        inc(V.tensor_scalar(T["CU" + B][:, :], T[offsets(x)][:, 0:NC // 8, :], float(M), None, OP.min), "cu" + B)
-
-    def acc(b):
-        return T.AC1[0:NQ, 4 * b - 4:4 * b, :] if b else T.AC0[0:NQ, 0:4, :]
-
-    def weigh(x):
-        if x <= state["weighed"]:
-            return
-        weigh(x - 1)
-        move(x)
-        state["weighed"] = x
-        b, t = seq[x]
-        B = str(b)
-        H = T["HW" + B]
-        wait(S, ("mm" if t == STEPS - 1 else "mn") + B)
-        if t:
-            wait(S, "ac" + B)
-        n = 192 if t == 0 else 96
-        inc(S.activation(H[0:NQ, 0:n], T["BK" + B][0:NQ, 8:8 + n // 8, :], FN.Relu), "hw" + B)
-        if (b, t) == (1, 0):
-            wait(PE, "pc", copied[2])
-        wait(PE, "hw" + B)
-        for h in range(n // 32):
-            ins = PE.matmul(acc(b), (T.S64, T.SEL, T.NS64)[h % 3][0:NQ, :], H[0:NQ, 32 * h:32 * h + 32],
-                            t == 0 and h == 0 and b < 2, h == 2 and t == STEPS - 1 and (b == 0 or x == last_other))
-        inc(ins, "ac" + B)
-
-    def send():
-        for b in range(1, NB):
-            wait(V, "ac%d" % b)
-        inc(V.tensor_copy(T.OUT[0:NQ, :], T.AC1[0:NQ, 0:12, :]), "oa")
-        wait(g, "oa")
-        g.remote_dma_fused([RemoteDMATransfer(dst_ids=[d], dma_engine_mask=m, remote_sem=sem["ra%d" % rank],
-                                              src=T.OUT[:, 32 * s - 32:32 * s], dst=T["L%d" % rank][:, :])
-                            for s, d, m in dests], local_sem=sem.rsent)
-
-    matrices = count["rs"]
-    before = {}
-    bring(0)
-    for x, (b, t) in enumerate(seq):
-        if b in before:
-            cast(before[b])
-            weigh(before[b])
-        before[b] = x
-        if (b, t) == (1, 0):
-            cast(x - 1)
-            bring(1)
-            bring(2)
-        tight = t > 0 and 2 <= x < len(seq) - 1 and seq[x + 1][0] == seq[x - 2][0] and state["cast"] < x - 2
-        gather(x, 0, CUT if tight else NC)
-        if x == 0:
-            later()
-        if x == last_other + 1:
-            send()
-        if tight:
-            cast(x - 2)
-            move(x - 1)
-            gather(x, CUT, NC)
-        turn(x)
-        if (b, t) == (1, 0):
-            bring(3)
-        move(x - 1)
-        cast(x - 2)
-        weigh(x if x == last_other else x - 2)
-    weigh(len(seq) - 1)
-
-    wait(V, "ac0")
-    inc(V.tensor_copy(T.OW[0:NQ, :], acc(0)), "ow")
-    for n in range(1, NB + 1):
-        if n < NB:
-            PE.wait_ge(sem["ra%d" % src[n]], EPD)
+            loaded = [("wld", count["wld"])] if t == 1 else []
+            cuts = (0, CUT, NC) if (b, t) == (0, STEPS - 1) else (0, NC)
+            for c0, c1 in zip(cuts, cuts[1:]):
+                task(("tests", b, t, c0), "V", [("cast", b, t - 1), ("keep", b), "later"], lambda c0=c0, c1=c1: V.tensor_tensor(
+                    C[:, 16 * c0:16 * c1], window.indirect(CU[:, c0:c1]), T.P[:, NL * b + 16 * c0:NL * b + 16 * c1], OP.is_gt), loaded)
+                task(("values", b, t, c0), "S", [("cast", b, t - 1), "later"], lambda c0=c0, c1=c1: S.activation(
+                    G[:, 16 * c0:16 * c1], window.indirect(CU[:, c0:c1]), FN.Identity, bias=col(27), scale=col(26)), loaded)
+            for name, made_by, X, R in (("turn G", "values", G, T.RA), ("turn C", "tests", C, T.RB)):
+                task((name, b, t), "PE", [(made_by, b, t, c0) for c0 in cuts[:-1]] + [("gate", b, t - 1), "more"],
+                     lambda X=X, R=R: turn(X, R), [("g", marked)] if t == 1 else [])
+            task(("turn N", b, t), "PE", [("turn G", b, t)], lambda: products(
+                lambda e: BK[0:NQ, 0:8, 0::2], lambda e: ID[0:NQ, 0:NQ], lambda e: IN[0:NQ, at:at + 32:4, e::2], 2,
+                *ends(("turn", b, t), 3)))
+        before = [("turn G", b, t), ("turn C", b, t)] + ([("turn N", b, t)] if t else [])
+        if t < STEPS - 1:
+            task(("max", b, t), "V", before, lambda: V.tensor_scalar(
+                IN[0:NQ, at:at + 32:4, :], BK[0:NQ, 0:8, :], -2048.0, None, OP.max), [("S", filled[-1])] if t == 0 else [])
+            early = (b, t) == (0, 0)
+            task(("place", b, t), "PE", [("gate" if early else "max", b, t)], lambda: products(
+                lambda n: offsets, lambda n: IN[0:NQ, at - n % 4:at + 32 - n % 4, n // 4::2], lambda n: ID[0:NQ, n % 4:NQ:4],
+                8, True, True))
+            task(("cast", b, t), "V", [("place", b, t)], lambda: V.tensor_scalar(CU[:, :], offsets, -1.0, None, OP.mult))
+            before = [("max" if early else "cast", b, t)]
+        n = (wide - 8) // 4
+        if t >= SUMMED:
+            H = T["HS%d" % b][:, 64 * (t - SUMMED):64 * (t - SUMMED) + 64]
         else:
-            wait(PE, "ow")
-        part = T["L%d" % src[n]] if n < NB else T.OW
-        ins = PE.matmul(T.RL[0:32, 0:NQ // 8, :], part[0:NQ, :], T.IDF[0:NQ, 0:NQ], n == 1, n == NB)
-    inc(ins, "fq")
-    wait(V, "fq")
-    inc(V.tensor_copy(T.YS[0:32, :], T.RL[0:32, 0:NQ // 8, :]), "hl")
+            H = T["HW%d" % b][:, 0:32 * n]
+            before = before + ([("weigh", b, t - 1)] if t else [])
+        task(("gate", b, t), "S", before, lambda: S.activation(H[0:NQ, :], BK[0:NQ, 8:wide, :], FN.Relu),
+             [("g", made)] if t == SUMMED else [])
+        if t < SUMMED:
+            task(("weigh", b, t), "PE", [("gate", b, t)] + ([("keep", 2), ("test", 2)] if b and t == 0 else []), lambda: products(
+                lambda h: acc, lambda h: weights[h % 2][0:NQ, 0:NQ], lambda h: H[0:NQ, 32 * h:32 * h + 32], n,
+                *ends(("acc", b > 0), SUMMED * (NB - 1 if b else 1))), [("g", scales)] if t == 0 else [])
+
+    def add(name, needs, H, h0, h1, waits=()):
+        task(name, "PE", needs, lambda: products(
+            lambda h: total, lambda h: H[0:NQ, 32 * (h0 + h):32 * (h0 + h) + 32], lambda h: weights[h % 2][0:NQ, 0:NQ],
+            h1 - h0, *ends("total", parts)), waits)
+
+    for b in range(NB):
+        source(b)
+        for t in range(STEPS):
+            step(b, t)
+    task("sums", "S", [("weigh", b, SUMMED - 1) for b in range(1, NB)],
+         lambda: S.activation(T.OUT[0:NQ, :], T.AC1[0:NQ, 0:12, :], FN.Copy), [("g", made)])
+    task("own sums", "S", [("weigh", 0, SUMMED - 1)], lambda: S.activation(T.OW[0:NQ, :], T.AC0[0:NQ, 0:4, :], FN.Copy))
+    task("send sums", "g", ["sums"], lambda: g.remote_dma_fused(
+        [to([s], EPD * n, EPD, "ra", T["L%d" % rank][:, :], T.OUT[:, 32 * s - 32:32 * s]) for n, s in enumerate(order)],
+        local_sem=sem.sent))
+    for n in range(NB):
+        task(("add sums", n), "PE", [] if n else ["own sums"], lambda n=n: PE.matmul(
+            total, (T["L%d" % src[n]] if n else T.OW)[0:NQ, :], T.IDF[0:NQ, :], *ends("total", parts)),
+            [("g", made)] + ([("ra%d" % src[n], EPD)] if n else []))
+    for t in range(SUMMED, STEPS):
+        add(("add own", t), [("gate", 0, t)], T.HS0, 2 * (t - SUMMED), 2 * (t - SUMMED) + 2)
+    for batches in ((1, 2), (3,)):
+        share = ALONE // len(batches)
+        task(("send", batches), "g", [("gate", s, t) for s in batches for t in range(SUMMED, STEPS)],
+             lambda batches=batches, share=share: g.remote_dma_fused(
+                 [to([s], share * n, share, "rb", T["HL%d" % rank][:, :], T["HS%d" % s][:, :]) for n, s in enumerate(batches)],
+                 local_sem=sem.sent))
+        for s in batches:
+            add(("add", s), [], T["HL%d" % src[NB - s]], 0, LEFT, [("rb%d" % src[NB - s], share)])
+    task("later", "V", [], later, [("V", bounds)])
+    task("more", "S", [], more, [("g", cleared)])
+    task("result", "V", [n for n in tasks if n[0][:3] == "add"], lambda: V.tensor_copy(T.YS[0:32, :], total))
+
+    done, waited = {}, {}
+
+    def put(*names):
+        for name in names:
+            if name in done or name not in tasks:
+                continue
+            q, needs, call, waits = tasks[name]
+            put(*needs)
+            for s, n in list(waits) + [(tasks[m][0], done[m]) for m in needs if (q, tasks[m][0]) != ("PE", "PE")]:
+                if waited.get((q, s), 0) < n:
+                    waited[q, s] = n
+                    wait(queue[q], s, n)
+            ins = call()
+            done[name] = 0 if q == "g" else inc(ins, q)
+
+    def gathers(b, t, c0=0):
+        put(("tests", b, t, c0), ("values", b, t, c0))
+
+    def turns(b, t):
+        put(("turn G", b, t), ("turn N", b, t), ("turn C", b, t))
+
+    put(("test", 0), ("keep", 0), "later")
+    turns(0, 0)
+    put(("bring", 1), ("bring", 2), ("bring", 3), ("place", 0, 0), "more", ("test", 1), ("keep", 3), ("keep", 1))
+    turns(1, 0)
+    put(("test", 2), ("keep", 2), ("cast", 0, 0))
+    turns(2, 0)
+    put(("place", 1, 0), ("test", 3))
+    turns(3, 0)
+    put(("place", 2, 0), ("cast", 1, 0), ("weigh", 0, 0))
+
+    seq = [(b, t) for t in range(STEPS - 1) for b in range(NB)]
+    for x in range(NB, len(seq)):
+        gathers(*seq[x])
+        turns(*seq[x])
+        put(("place",) + seq[x - 1], ("cast",) + seq[x - 2], ("gate",) + seq[x - 3], ("weigh",) + seq[x - 3])
+
+    E, D = STEPS - 1, STEPS - 2
+    gathers(0, E)
+    put("send sums", ("place", 3, D), ("cast", 2, D), ("gate", 1, D))
+    gathers(1, E)
+    turns(1, E)
+    put(("cast", 3, D), ("gate", 2, D))
+    gathers(2, E)
+    put(("gate", 3, D))
+    turns(2, E)
+    gathers(3, E)
+    put(("send", (1, 2)))
+    turns(3, E)
+    put("own sums")
+    gathers(0, E, CUT)
+    put(("send", (3,)), *[("add sums", n) for n in range(NB)])
+    turns(0, E)
+    put(("add own", D), ("add", 1), ("add", 2), ("add own", E), ("add", 3), "result")
+
     for e, q in enumerate((Y, S)):
-        wait(q, "hl")
+        wait(q, "V")
         inc(q.dma_start(T.y[e::2, :], T.YS[e:32:2, :]), "yd", 16)
-    wait(Y, "yd")
-    g.wait_ge(sem.psent, 3 * EPD)
-    g.wait_ge(sem.rsent, 3 * EPD)
+    for name in ("S", "PE", "g", "yd"):
+        wait(Y, name)
+    g.wait_ge(sem.sent, 3 * EPD + 3 * ALONE)

from concourse.bass import DstId, RemoteDMATransfer
from concourse.mybir import dt, AluOpType, AxisListType, ActivationFunctionType

OP = AluOpType
FN = ActivationFunctionType
NB = 4
NL = 384
NQ = NL // 4
NC = NL // 16
STEPS = 15
SUMMED = 13
LEFT = 2 * (STEPS - SUMMED)
M = 4096
WIN = 4104
WHOLE = 768
EARLY = 896
FILLS = ((896, 1920), (1920, 2944), (2944, 3968), (3968, M))
ROW_ONE, ROW_LO = 9, 12
EPD = 4
ALONE = 16
BIG = 8192.0
SHIFT = -1536
COPIED = (3,)
CUT = 12

SCRATCH = {
    "W": ("sbuf", [128, WIN], "int32"),
    "XI": ("sbuf", [128, 192], "int32"),
    "XS": ("sbuf", [128, 192], "int32"),
    "XF": ("sbuf", [128, 192], "float16"),
    "XW": ("sbuf", [128, 256], "int32"),
    "LO": ("sbuf", [128, 256], "int32"),
    "NN": ("sbuf", [128, 2], "int32"),
    "NH": ("sbuf", [128, 4], "int32"),
    "P": ("sbuf", [128, NB * NL], "float32"),
    "KI": ("sbuf", [128, 4], "int32"),
    "CI": ("sbuf", [128, 16], "int32"),
    "CH": ("sbuf", [128, 16], "int32"),
    "SI": ("sbuf", [128, 8, 16], "int32"),
    "SP": ("sbuf", [128, 16, 16], "float16"),
    "KF": ("sbuf", [128, 64], "float32"),
    "OH": ("sbuf", [128, 16], "float32"),
    "B8": ("sbuf", [128, 16], "float32"),
    "IDF": ("sbuf", [128, 96], "float32"),
    "ID": ("sbuf", [128, 128], "float16"),
    "ZT": ("sbuf", [128, 128], "float16"),
    "UP": ("sbuf", [128, 96], "float16"),
    "DOWN": ("sbuf", [128, 96], "float16"),
    "RA": ("sbuf", [128, 32], "float16"),
    "RB": ("sbuf", [128, 32], "float16"),
    "RS": ("sbuf", [128, 48], "float16"),
    "RD": ("sbuf", [128, 48], "float16"),
    "IN": ("sbuf", [128, 32 * NB + 4, 8], "float16"),
    "OUT": ("sbuf", [128, 96], "float32"),
    "OW": ("sbuf", [128, 32], "float32"),
    "YS": ("sbuf", [128, 96], "float32"),
    "CP": ("psum", [128, 64, 8], "float32"),
    "RL": ("psum", [128, 64, 8], "float32"),
    "AC0": ("psum", [128, 64, 8], "float32"),
    "AC1": ("psum", [128, 64, 8], "float32"),
}
for _b in range(NB):
    SCRATCH["C%d" % _b] = ("sbuf", [128, NL], "float16")
    SCRATCH["G%d" % _b] = ("sbuf", [128, NL], "float16")
    SCRATCH["CU%d" % _b] = ("sbuf", [128, NC], "uint16")
    SCRATCH["HW%d" % _b] = ("sbuf", [128, 128], "float16")
    SCRATCH["BK%d" % _b] = ("psum", [128, 64, 8], "float32")
    SCRATCH["XR%d" % _b] = ("sbuf", [128, 192], "float16")
    SCRATCH["L%d" % _b] = ("sbuf", [128, 32], "float32")
    SCRATCH["HS%d" % _b] = ("sbuf", [128, 32 * LEFT], "float16")
    SCRATCH["HL%d" % _b] = ("sbuf", [128, 32 * LEFT], "float16")

SEMAPHORES = ["xld", "xwld", "nld", "w0", "wld", "V", "S", "PE", "g", "sent", "yd"]
for _b in range(NB):
    SEMAPHORES += ["%s%d" % (n, _b) for n in ("pa", "ra", "rb")]


def rank_program(g, core, T, topo):
    rank = T.rank_of(core)
    if rank is None:
        return
    sem = T.sem
    V, S, PE, Y = g.vector, g.scalar, g.tensor, g.sync
    queue = {"V": V, "S": S, "PE": PE, "g": g}
    src = [(rank + s) % NB for s in range(NB)]
    count = {}

    def inc(ins, name, n=1):
        ins.then_inc(sem[name], n)
        count[name] = count.get(name, 0) + n
        return count[name]

    def wait(q, name, n=None):
        q.wait_ge(sem[name], count[name] if n is None else n)

    def to(sources, a, n, name, out, in_):
        cores = [T.cores[src[s]] for s in sources]
        e = [x for x in topo.engines(core, cores[0]) if all(x in topo.engines(core, c) for c in cores)]
        return RemoteDMATransfer(dst_ids=[DstId(rid=topo.addr(c)[0], pnc=topo.addr(c)[1]) for c in cores],
                                 dma_engine_mask=sum(1 << x for x in (e[0::2] + e[1::2])[a:a + n]),
                                 remote_sem=sem["%s%d" % (name, rank)], srcs=[in_], dsts=[out] * len(cores))

    order = sorted(range(1, NB), key=lambda s: topo.die(T.cores[src[s]]) == topo.die(core))
    KF, OH, ID, zeros = T.KF, T.OH, T.ID, T.ZT

    def col(j):
        return KF[:, j:j + 1]

    def oh(r):
        return OH[:, r:r + 1]

    def v(ins):
        return inc(ins, "V")

    def scaled(out, mask, c):
        return inc(S.activation(out, mask, FN.Copy, scale=c), "S")

    def block(R, n):
        return R[:, n:16:2] if n < 2 else R[:, 8 * n:8 * n + 8]

    def mark(out, in_, step, base, value):
        return inc(g.affine_select(out, in_, [[-step, out.shape[-1]]], OP.not_equal, value, -base, 1), "g")

    inc(Y.dma_start(T.XI[0:48, :], T.pts[:, :]), "xld", 16)
    inc(S.dma_start(T.XI[64:112, :], T.pts[:, :]), "xld", 16)
    inc(Y.dma_start(T.XW[:, :], T.nodes[7::16, :]), "xwld", 16)

    zero = v(V.memset(T.IN[:, :, :], 0.0))
    pad = v(V.memset(T.XF[:, :], 0.0))
    blank = v(V.memset(zeros[:, :], 0.0))

    inc(g.iota(T.KI[:, 0:1], [[1, 1]], 0, 1), "g")
    first = inc(g.iota(T.CI[:, :], [[1, 16]], 0, 0), "g")
    inc(g.iota(T.CH[:, :], [[0, 2], [1, 8]], 0, 0), "g")
    inc(g.iota(T.SI[:, :, 0:12], [[6, 8], [0, 4], [2, 3]], 0, 0), "g")
    patterns = inc(g.iota(T.SI[:, :, 12:16], [[0, 32]], 999, 0), "g")
    wait(g, "V", blank)
    ident = mark(ID[:, :], zeros[:, :], 1, 0, 1.0)
    cleared = mark(T.RB[:, 0:16], zeros[:, 0:16], 0, -1, 0.0)
    if EARLY > WHOLE:
        inc(g.iota(T.W[:, WHOLE:EARLY], [[0, EARLY - WHOLE]], 0, 0), "g")

    inc(Y.dma_start(T.NN[6:128, :], T.nodes[0:122, 0:2]), "nld", 16)
    inc(Y.dma_start(T.NN[0:6, :], T.nodes[0:6, 0:2]), "nld", 16)
    inc(Y.dma_start(T.W[:, 0:WHOLE], T.nodes[:, 0:WHOLE]), "w0", 16)
    wait(S, "V", zero)
    filled = [inc(S.activation(T.W[:, lo:hi], T.IN[:, 0:(hi - lo) // 8, :], FN.Copy), "S") for lo, hi in FILLS]
    wait(Y, "g")
    for c, lo, hi in ((0, WHOLE, FILLS[0][1]), (-1, FILLS[0][1], M)):
        wait(Y, "S", filled[c])
        for a in range(8):
            inc(Y.dma_start(T.W[a::16, lo:hi], T.nodes[a::16, lo:hi]), "wld", 16)

    wait(V, "g", first)
    for j, (c, op) in enumerate(((15, OP.bitwise_and), (4, OP.arith_shift_right), (63, OP.bitwise_and))):
        n = v(V.tensor_scalar(T.KI[:, 1 + j:2 + j], T.KI[:, 0:1], c, None, op))
    wait(V, "xld")
    split = v(V.tensor_scalar(T.XS[64:112, :], T.XI[64:112, :], 2047, None, OP.bitwise_and))
    wait(V, "V", pad)
    v(V.tensor_scalar(T.XF[0:48, :], T.XI[0:48, :], 2.0 ** -11, SHIFT - 0.5 + 2.0 ** -12, OP.mult, OP.add))
    wait(V, "V", n)
    n = v(V.tensor_copy(KF[:, 1:4], T.KI[:, 1:4]))
    wait(V, "V", split)
    points = v(V.tensor_scalar(T.XF[64:112, :], T.XS[64:112, :], 2.0 ** -11, None, OP.mult))
    wait(V, "V", n)
    r_, g_ = col(1), col(2)
    v(V.tensor_scalar(OH[:, :], T.CI[:, :], r_, None, OP.is_equal))
    n = v(V.tensor_scalar(KF[:, 4:8], T.CI[:, 3:13:3], r_, None, OP.is_gt))
    wait(V, "g", patterns)
    v(V.tensor_scalar(T.B8[:, :], T.CH[:, :], g_, None, OP.is_equal))
    for h in range(2):
        place = v(V.tensor_scalar(T.SP[:, 8 * h:8 * h + 8, :], T.SI[:, :, :], float(h), col(3), OP.add, OP.is_equal))
    wait(V, "V", n)
    lt3, lt6, lt9, lt12 = col(4), col(5), col(6), col(7)
    v(V.tensor_scalar(col(8), lt3, 2.0, lt6, OP.mult, OP.subtract))
    v(V.tensor_scalar(col(9), lt3, lt6, lt9, OP.subtract, OP.add))
    v(V.tensor_scalar(col(10), lt12, lt6, None, OP.subtract))
    n = v(V.tensor_scalar(KF[:, 12:14], T.CI[:, 3:7:3], oh(15), -BIG, OP.mult, OP.mult))
    wait(V, "xwld")
    v(V.tensor_scalar(T.LO[:, :], T.XW[:, :], 127, None, OP.bitwise_and))
    wait(V, "V", n)
    v(V.tensor_scalar(col(23), col(9), 2.0, lt12, OP.mult, OP.subtract))
    v(V.tensor_scalar(col(30), lt12, -2048.0 * SHIFT, -0.5, OP.mult, OP.add))
    n = v(V.tensor_scalar(col(25), col(8), -BIG, col(12), OP.mult, OP.add))
    wait(V, "nld")
    v(V.tensor_scalar(T.NH[:, 0:2], T.NN[:, :], 7, None, OP.arith_shift_right))
    halves = v(V.tensor_scalar(T.NH[:, 2:4], T.NN[:, :], 127, None, OP.bitwise_and))
    wait(V, "V", n)
    n = v(V.tensor_scalar(col(28), col(23), 0.5, col(30), OP.mult, OP.add))
    fixed = v(V.tensor_scalar(col(29), col(23), -BIG, col(13), OP.mult, OP.add))
    v(V.tensor_scalar(col(40), T.NN[:, 1:2], -2050.0, None, OP.add))
    wait(V, "V", halves)
    v(V.tensor_scalar(KF[:, 42:44], T.NH[:, 2:4], 512.0, None, OP.add))
    high = v(V.tensor_scalar(KF[:, 46:48], T.NH[:, 0:2], -1.0, 4.0, OP.mult, OP.add))
    wait(V, "V", n)
    wait(V, "w0")
    read = v(V.tensor_scalar(col(33), T.W[:, 0:1], lt6, col(28), OP.mult, OP.subtract))
    v(V.tensor_scalar(col(41), T.NN[:, 1:2], -1.0, 2048.0, OP.mult, OP.add))
    v(V.tensor_scalar(col(26), lt6, -1 / 128, 1 / 128, OP.mult, OP.add))
    wait(V, "V", high)
    cols = v(V.tensor_tensor(KF[:, 44:46], KF[:, 42:44], KF[:, 46:48], OP.add))
    v(V.tensor_scalar(col(27), oh(7), 16 + SHIFT - 0.5 + 2.0 ** -8, -16.0, OP.mult, OP.add))
    wait(V, "V", read)
    bounds = v(V.tensor_scalar(col(34), T.NN[:, 1:2], col(10), col(33), OP.mult, OP.add))

    def later():
        V.tensor_scalar(col(32), col(34), col(28), None, OP.add)
        return V.tensor_scalar(T.W[:, M:M + 1], col(8), 2.0 ** 22, float(M), OP.mult, OP.add)

    wait(g, "V", points)
    g.remote_dma_fused([to(range(NB - 1, 0, -1), 0, ALONE, "pa", T["XR%d" % rank][:, :], T.XF[:, :])], local_sem=sem.sent)
    for out, c in ((T.UP, 129.0), (T.DOWN, -128.0)):
        scales = mark(out[:, :], zeros[:, 0:NQ], 1, 0, c)
    terms = (((6, 128.0), (ROW_ONE, 1 / 16)), ((6, -128.0),), ((ROW_LO, 128.0), (ROW_ONE, -(2048 + 512) / 16)),
             ((ROW_LO, 128.0), (7, -1.0), (ROW_ONE, -(2048 + 516 + SHIFT) / 16)))
    for k in range(3):
        if k:
            wait(g, "g")
        for n, rows_ in enumerate(terms):
            if k < len(rows_):
                marked = mark(block(T.RA, n), block(T.RA, n) if k else zeros[:, 0:8], 16, *rows_[k])
    for out in (T.IDF, T.OUT):
        inc(g.iota(out[:, :], [[0, 96]], 0, 0, allow_small_or_imprecise_dtypes=True), "g")
    for b in range(1, NB):
        mark(T["HS%d" % b][:, :], zeros[:, 0:32 * LEFT], 0, -1, 0.0)
    wait(g, "g")
    made = mark(T.IDF[:, :], T.IDF[:, :], 1, 0, 1.0)

    wait(Y, "V", read)
    inc(Y.dma_start(T.W[ROW_LO::16, 0:M], T.LO[:, :]), "wld", 16)

    wait(S, "V", fixed)
    scaled(block(T.RS, 0), T.B8[:, 0:8], col(29))
    scaled(block(T.RS, 1), T.B8[:, 0:8], col(25))
    scaled(T.RS[:, 16:32], T.B8[:, :], col(29))
    scaled(T.RS[:, 32:48], T.B8[:, :], col(25))
    wait(S, "V", cols)
    wait(S, "g", ident)
    for n, (row, c) in enumerate(((12, 40), (12, 41), (13, 43), (13, 45), (13, 42), (13, 44))):
        matrices = scaled(block(T.RD, n), ID[:, row::16], col(c))

    def more():
        S.activation(block(T.RB, 0), T.B8[:, 0:8], FN.Copy, scale=col(25))
        return S.activation(T.RB[:, 16:32], T.B8[:, :], FN.Copy, scale=col(25))

    tasks, group = {}, {}

    def task(name, q, needs, call, waits=()):
        tasks[name] = (q, needs, call, waits)

    def ends(name, n):
        group[name] = group.get(name, 0) + 1
        return group[name] == 1, group[name] == n

    def products(out, lhs, rhs, n, start, stop):
        for i in range(n):
            ins = PE.matmul(out(i), lhs(i), rhs(i), start and i == 0, stop and i == n - 1)
        return ins

    land = [T.CP, T.RL, T.AC1, T.CP]
    window = T.W[:, 0:M + 1]
    total = T.RL[0:32, 0:NQ // 8, :]
    weights = (T.UP, T.DOWN)
    parts = 2 * NB - 1 + STEPS - SUMMED

    def source(b):
        X, C, P = T.XF if b == 0 else T["XR%d" % src[b]], T["C%d" % b], T.P[:, NL * b:NL * b + NL]
        task(("bring", b), "PE", [("keep", 0)] if b == NB - 1 else [], lambda: products(
            lambda u: land[b][:, 0:NL // 8, u::4], lambda u: T.SP[:, 8 * (u // 2):8 * (u // 2) + 8, :],
            lambda u: X[:, NQ * (u % 2):NQ * (u % 2) + NQ], 4, True, True), [("pa%d" % src[b], ALONE)] if b else [("V", place)])
        copied = b in COPIED
        task(("keep", b), "S", [("bring" if copied else "test", b)], lambda: S.activation(
            P, land[b][:, 0:NL // 8, :], FN.Identity, bias=col(28), scale=2048.0))
        if copied:
            task(("test", b), "V", [("keep", b), "later"], lambda: V.tensor_scalar(C[:, :], P, col(32), None, OP.is_lt))
        else:
            task(("test", b), "V", [("bring", b)], lambda: V.tensor_scalar(
                C[:, :], land[b][:, 0:NL // 8, :], 2048.0, col(34), OP.mult, OP.is_lt), [("V", bounds)])

    def step(b, t):
        at = 32 * b + 3
        C, G, CU, BK, IN = T["C%d" % b], T["G%d" % b], T["CU%d" % b], T["BK%d" % b], T.IN
        acc = T.AC1[0:NQ, 4 * b - 4:4 * b, :] if b else T.AC0[0:NQ, 0:4, :]
        wide = 16 if t else 24
        offsets = BK[:, 32:32 + NC // 8, :]

        def turn(X, R):
            return products(lambda i: BK[0:NQ, 0:wide, 2 * i:2 * i + 2], lambda i: X[:, i::4], lambda i: R[:, :], 4,
                            *ends(("turn", b, t), 3 if t else 2))

        if t == 0:
            for name, R in (("turn G", T.RD), ("turn C", T.RS)):
                task((name, b, 0), "PE", [("test", b)], lambda R=R: turn(C, R), [("S", matrices)])
        else:
            loaded = [("wld", count["wld"])] if t == 1 else []
            cuts = (0, CUT, NC) if (b, t) == (0, STEPS - 1) else (0, NC)
            for c0, c1 in zip(cuts, cuts[1:]):
                task(("tests", b, t, c0), "V", [("cast", b, t - 1), ("keep", b), "later"], lambda c0=c0, c1=c1: V.tensor_tensor(
                    C[:, 16 * c0:16 * c1], window.indirect(CU[:, c0:c1]), T.P[:, NL * b + 16 * c0:NL * b + 16 * c1], OP.is_gt), loaded)
                task(("values", b, t, c0), "S", [("cast", b, t - 1), "later"], lambda c0=c0, c1=c1: S.activation(
                    G[:, 16 * c0:16 * c1], window.indirect(CU[:, c0:c1]), FN.Identity, bias=col(27), scale=col(26)), loaded)
            for name, made_by, X, R in (("turn G", "values", G, T.RA), ("turn C", "tests", C, T.RB)):
                task((name, b, t), "PE", [(made_by, b, t, c0) for c0 in cuts[:-1]] + [("gate", b, t - 1), "more"],
                     lambda X=X, R=R: turn(X, R), [("g", marked)] if t == 1 else [])
            task(("turn N", b, t), "PE", [("turn G", b, t)], lambda: products(
                lambda e: BK[0:NQ, 0:8, 0::2], lambda e: ID[0:NQ, 0:NQ], lambda e: IN[0:NQ, at:at + 32:4, e::2], 2,
                *ends(("turn", b, t), 3)))
        before = [("turn G", b, t), ("turn C", b, t)] + ([("turn N", b, t)] if t else [])
        if t < STEPS - 1:
            task(("max", b, t), "V", before, lambda: V.tensor_scalar(
                IN[0:NQ, at:at + 32:4, :], BK[0:NQ, 0:8, :], -2048.0, None, OP.max), [("S", filled[-1])] if t == 0 else [])
            early = (b, t) == (0, 0)
            task(("place", b, t), "PE", [("gate" if early else "max", b, t)], lambda: products(
                lambda n: offsets, lambda n: IN[0:NQ, at - n % 4:at + 32 - n % 4, n // 4::2], lambda n: ID[0:NQ, n % 4:NQ:4],
                8, True, True))
            task(("cast", b, t), "V", [("place", b, t)], lambda: V.tensor_scalar(CU[:, :], offsets, -1.0, None, OP.mult))
            before = [("max" if early else "cast", b, t)]
        n = (wide - 8) // 4
        if t >= SUMMED:
            H = T["HS%d" % b][:, 64 * (t - SUMMED):64 * (t - SUMMED) + 64]
        else:
            H = T["HW%d" % b][:, 0:32 * n]
            before = before + ([("weigh", b, t - 1)] if t else [])
        task(("gate", b, t), "S", before, lambda: S.activation(H[0:NQ, :], BK[0:NQ, 8:wide, :], FN.Relu),
             [("g", made)] if t == SUMMED else [])
        if t < SUMMED:
            task(("weigh", b, t), "PE", [("gate", b, t)] + ([("keep", 2), ("test", 2)] if b and t == 0 else []), lambda: products(
                lambda h: acc, lambda h: weights[h % 2][0:NQ, 0:NQ], lambda h: H[0:NQ, 32 * h:32 * h + 32], n,
                *ends(("acc", b > 0), SUMMED * (NB - 1 if b else 1))), [("g", scales)] if t == 0 else [])

    def add(name, needs, H, h0, h1, waits=()):
        task(name, "PE", needs, lambda: products(
            lambda h: total, lambda h: H[0:NQ, 32 * (h0 + h):32 * (h0 + h) + 32], lambda h: weights[h % 2][0:NQ, 0:NQ],
            h1 - h0, *ends("total", parts)), waits)

    for b in range(NB):
        source(b)
        for t in range(STEPS):
            step(b, t)
    task("sums", "S", [("weigh", b, SUMMED - 1) for b in range(1, NB)],
         lambda: S.activation(T.OUT[0:NQ, :], T.AC1[0:NQ, 0:12, :], FN.Copy), [("g", made)])
    task("own sums", "S", [("weigh", 0, SUMMED - 1)], lambda: S.activation(T.OW[0:NQ, :], T.AC0[0:NQ, 0:4, :], FN.Copy))
    task("send sums", "g", ["sums"], lambda: g.remote_dma_fused(
        [to([s], EPD * n, EPD, "ra", T["L%d" % rank][:, :], T.OUT[:, 32 * s - 32:32 * s]) for n, s in enumerate(order)],
        local_sem=sem.sent))
    for n in range(NB):
        task(("add sums", n), "PE", [] if n else ["own sums"], lambda n=n: PE.matmul(
            total, (T["L%d" % src[n]] if n else T.OW)[0:NQ, :], T.IDF[0:NQ, :], *ends("total", parts)),
            [("g", made)] + ([("ra%d" % src[n], EPD)] if n else []))
    for t in range(SUMMED, STEPS):
        add(("add own", t), [("gate", 0, t)], T.HS0, 2 * (t - SUMMED), 2 * (t - SUMMED) + 2)
    for batches in ((1, 2), (3,)):
        share = ALONE // len(batches)
        task(("send", batches), "g", [("gate", s, t) for s in batches for t in range(SUMMED, STEPS)],
             lambda batches=batches, share=share: g.remote_dma_fused(
                 [to([s], share * n, share, "rb", T["HL%d" % rank][:, :], T["HS%d" % s][:, :]) for n, s in enumerate(batches)],
                 local_sem=sem.sent))
        for s in batches:
            add(("add", s), [], T["HL%d" % src[NB - s]], 0, LEFT, [("rb%d" % src[NB - s], share)])
    task("later", "V", [], later, [("V", bounds)])
    task("more", "S", [], more, [("g", cleared)])
    task("result", "V", [n for n in tasks if n[0][:3] == "add"], lambda: V.tensor_copy(T.YS[0:32, :], total))

    done, waited = {}, {}

    def put(*names):
        for name in names:
            if name in done or name not in tasks:
                continue
            q, needs, call, waits = tasks[name]
            put(*needs)
            for s, n in list(waits) + [(tasks[m][0], done[m]) for m in needs if (q, tasks[m][0]) != ("PE", "PE")]:
                if waited.get((q, s), 0) < n:
                    waited[q, s] = n
                    wait(queue[q], s, n)
            ins = call()
            done[name] = 0 if q == "g" else inc(ins, q)

    def gathers(b, t, c0=0):
        put(("tests", b, t, c0), ("values", b, t, c0))

    def turns(b, t):
        put(("turn G", b, t), ("turn N", b, t), ("turn C", b, t))

    put(("test", 0), ("keep", 0), "later")
    turns(0, 0)
    put(("bring", 1), ("bring", 2), ("bring", 3), ("place", 0, 0), "more", ("test", 1), ("keep", 3), ("keep", 1))
    turns(1, 0)
    put(("test", 2), ("keep", 2), ("cast", 0, 0))
    turns(2, 0)
    put(("place", 1, 0), ("test", 3))
    turns(3, 0)
    put(("place", 2, 0), ("cast", 1, 0), ("weigh", 0, 0))

    seq = [(b, t) for t in range(STEPS - 1) for b in range(NB)]
    for x in range(NB, len(seq)):
        gathers(*seq[x])
        turns(*seq[x])
        put(("place",) + seq[x - 1], ("cast",) + seq[x - 2], ("gate",) + seq[x - 3], ("weigh",) + seq[x - 3])

    E, D = STEPS - 1, STEPS - 2
    gathers(0, E)
    put("send sums", ("place", 3, D), ("cast", 2, D), ("gate", 1, D))
    gathers(1, E)
    turns(1, E)
    put(("cast", 3, D), ("gate", 2, D))
    gathers(2, E)
    put(("gate", 3, D))
    turns(2, E)
    gathers(3, E)
    put(("send", (1, 2)))
    turns(3, E)
    put("own sums")
    gathers(0, E, CUT)
    put(("send", (3,)), *[("add sums", n) for n in range(NB)])
    turns(0, E)
    put(("add own", D), ("add", 1), ("add", 2), ("add own", E), ("add", 3), "result")

    for e, q in enumerate((Y, S)):
        wait(q, "V")
        inc(q.dma_start(T.y[e::2, :], T.YS[e:32:2, :]), "yd", 16)
    for name in ("S", "PE", "g", "yd"):
        wait(Y, name)
    g.wait_ge(sem.sent, 3 * EPD + 3 * ALONE)
